import numpy as np, ml_dtypes
CORES = [3,5,19,21,35,37,51,53,67,69]
N = 10
RM, R, T = 262144, 8192, 512
CAPP = 128
def entries(a): return a.T.reshape(-1)
def pack(v, P): return np.ascontiguousarray(np.asarray(v, np.int32).reshape(-1, P).T)
def owners(rng, how):
    if how == "alike": return np.stack([rng.permutation(np.repeat(rng.permutation(N)[:T // CAPP], CAPP)) for r in range(N)])
    if how == "full": p = np.repeat(rng.permutation(N)[:T // CAPP], CAPP); return np.stack([rng.permutation(p) for r in range(N)])
    return np.stack([rng.permutation(np.repeat(np.arange(N), CAPP))[:T] for r in range(N)])
def lists(rng, how):
    M = rng.integers(0, N * R, N * RM)
    O1 = owners(rng, how); O2 = rng.permutation(N)[O1] if how in ("alike", "full") else owners(rng, "uniform")
    sl = np.stack([1 + rng.permutation(RM - 2)[:N * T] for o in range(N)])
    if how == "edge": sl[:, 0] = 0; sl[:, 1] = RM - 1
    I = np.zeros((N, T), np.int64); took = np.zeros(N, np.int64)
    for r in range(N):
        for o in range(N): m = np.nonzero(O1[r] == o)[0]; I[r, m] = RM * o + sl[o, took[o]:took[o] + len(m)]; took[o] += len(m)
    A = R * O2 + (np.where(rng.random((N, T)) < 0.5, 0, R - 1) if how == "edge" else rng.integers(0, R, (N, T)))
    if how == "alike": I = RM * O1 + sl[O1, 0]; A = R * O2 + rng.integers(0, R, N)[O1]
    M[I.reshape(-1)] = A.reshape(-1)
    if how == "sorted": I = np.sort(I, axis=1)
    if how == "full":
        I[1::3] = np.sort(I[1::3], axis=1); I[2::3] = np.sort(I[2::3], axis=1).reshape(-1, 16, T // 16).transpose(0, 2, 1).reshape(-1, T)
    return {"mp": np.stack([pack(m, 16) for m in M.reshape(N, RM)]), "idx": np.stack([pack(i, 16) for i in I])}
def setup_inputs(rng):
    return dict({"tab": rng.standard_normal((N, 128, R), dtype=np.float32).astype(ml_dtypes.bfloat16)}, **lists(rng, "uniform"))
def setup_inputs_alike(rng):
    d = setup_inputs(rng); d.update(lists(rng, "alike"))
    for k in ("tab",): d[k] = (d[k].astype(np.float32) * 1048576.0).astype(d[k].dtype)
    return d
def setup_inputs_edge(rng):
    d = setup_inputs(rng); d.update(lists(rng, "edge"))
    for k in ("tab",): d[k] = (d[k].astype(np.float32) * (1 / 1024.0)).astype(d[k].dtype)
    return d
def setup_inputs_full(rng):
    d = setup_inputs(rng); d.update(lists(rng, "full"))
    return d
def setup_inputs_sorted(rng):
    d = setup_inputs(rng); d.update(lists(rng, "sorted"))
    return d
def check_inputs(x):
    bad = []
    if x["mp"].min() < 0 or x["mp"].max() >= N * R: bad.append("mp out of range")
    if x["idx"].min() < 0 or x["idx"].max() >= N * RM: bad.append("idx out of range")
    M = np.concatenate([entries(m) for m in x["mp"]])
    if max(int(np.bincount(entries(a) // RM, minlength=N).max()) for a in x["idx"]) > CAPP: bad.append("more than CAPP entries of a list point into one rank's part of the map")
    if max(int(np.bincount(M[entries(a)] // R, minlength=N).max()) for a in x["idx"]) > CAPP: bad.append("more than CAPP entries of a list have map values in one rank's part of the table")
    return bad
def reference(tab, mp, idx):
    A = np.concatenate(list(tab), axis=1)
    M = np.concatenate([entries(m) for m in mp])
    return {"y": np.stack([A[:, M[entries(idx[r])]] for r in range(N)])}

@@ -1,0 +1,480 @@
+import numpy as np
+from concourse.bass import DstId, RemoteDMATransfer
+from concourse.mybir import dt, AluOpType, ActivationFunctionType
+
+LANE_M = True
+LANE_T = True
+MC = 4
+MW = 2048 // MC
+NM = 4097 if LANE_M else 2049
+NT = 16384 if LANE_T else 8192
+NEV = 140
+F32, BF, FP, I32, U16 = "float32", "bfloat16", "float16", "int32", "uint16"
+
+
+def _sb(n, d):
+    return ("sbuf", [128, n], d)
+
+
+SCRATCH = {
+    "winM": _sb(NM + 3, I32), "winT": _sb(NT, BF), "zero": _sb(4, I32), "ix": _sb(4, I32),
+    "row": _sb(256, BF),
+    "lA": _sb(512, FP), "rA": _sb(320, FP), "lF": _sb(128, FP), "rF": _sb(32, FP),
+    "lQ": _sb(512, BF), "rQ": _sb(640, BF), "Tk": _sb(512, BF), "lC": _sb(512, BF), "rC": _sb(640, BF),
+    "rep": _sb(4, U16), "repF": _sb(2, U16), "offF": _sb(32, U16),
+    "sendA": _sb(80, U16), "offA": _sb(80, U16), "sendC": _sb(80, U16), "offC": _sb(80, U16),
+    "G": _sb(1280, F32), "sendB": _sb(160, F32), "landB": _sb(160, F32),
+    "sendD": _sb(1280, BF), "landD": _sb(1280, BF), "yo": _sb(512, BF),
+}
+PACK = {
+    ("pf", F32): [("dP", 4), ("dC", 4), ("delta", 4), ("g16", 4), ("c16A", 4), ("hA", 4), ("mcol", 4), ("a0", 4), ("u128", 4),
+                  ("u8", 4), ("pl0", 4), ("pl", 4), ("n1", 4), ("n2", 4), ("qc", 4), ("tU", 4), ("lc", 4), ("hi2", 4), ("lo2", 4),
+                  ("c16C", 4), ("sC", 4), ("slotC", 4), ("PF", 4), ("S16", 16), ("Z0", 32), ("RA", 64), ("SA", 64), ("RC", 64),
+                  ("SC", 64), ("X", 160), ("SX", 160), ("D1", 128), ("SD", 128), ("mask2", 128)],
+    ("pi", I32): [("bI", 4), ("iPart", 4), ("iCl", 4), ("iCh", 4), ("iG", 4), ("iNl", 4), ("iNh", 4), ("REP", 4), ("PI", 2),
+                  ("P3", 2), ("P15", 1), ("P7", 1), ("PS3", 1)],
+    ("pb", BF): [("I16", 160), ("I128", 128), ("JK", 128), ("N16", 80), ("I160", 160), ("TC", 64), ("I32r", 128), ("Z4", 32),
+                 ("ones", 128), ("Lt", 128), ("Lu", 128), ("Lp", 128), ("ident", 128), ("rst", 160), ("rst32", 128),
+                 ("I16m", 128), ("U128", 32), ("EA", 64), ("EC", 64), ("HL", 32)],
+}
+PLACE = {}
+for (_b, _d), _l in PACK.items():
+    _o = 0
+    for _n, _w in _l:
+        PLACE[_n] = (_b, _o, _w)
+        _o += _w
+    SCRATCH[_b] = _sb(_o, _d)
+for _k in (0, 1, 2, 3, 4, 5, 7):
+    SCRATCH["b%d" % _k] = ("psum", [128, 512], F32)
+SCRATCH["b6"] = ("psum", [128, 1024], BF)
+SEMAPHORES = ["mArr", "aArr", "bArr", "tArr", "cArr", "dArr"] + ["e%d" % i for i in range(NEV)]
+
+OP = AluOpType
+SR, AND = OP.logical_shift_right, OP.bitwise_and
+COPY = ActivationFunctionType.Copy
+RND = 1.5 * 2.0 ** 23
+
+
+def rank_program(g, core, T, topo):
+    rank = T.rank_of(core)
+    if rank is None:
+        return
+    cores = T.cores
+    v, pe, sc, sy = g.vector, g.tensor, g.scalar, g.sync
+    Q = {"v": v, "p": pe, "a": sc, "y": sy, "g": g}
+    chips = []
+    for c in cores:
+        if topo.chip(c) not in chips:
+            chips.append(topo.chip(c))
+    partner = [c for c in cores if c != core and topo.chip(c) == topo.chip(core)][0]
+    part = rank % 2
+
+    def A(name, a=0, b=None, step=1):
+        buf, o, w = PLACE[name]
+        b = w if b is None else b
+        return T[buf][:, o + a:o + b:step] if step > 1 else T[buf][:, o + a:o + b]
+
+    def servers(lane):
+        if not lane:
+            return list(cores)
+        return [[c for c in cores if topo.chip(c) == ch and topo.die(c) == topo.die(core)][0] for ch in chips]
+
+    sM, sT = servers(LANE_M), servers(LANE_T)
+    meM, meT = sM.index(core), sT.index(core)
+    szM, szT = 1280 // len(sM), 1280 // len(sT)
+
+    groups, waited = [], {}
+
+    def ev(sem=None):
+        e = {"s": sem if sem is not None else T.sem["e%d" % len(groups)], "n": 0, "k": len(groups)}
+        groups.append(e)
+        return e
+
+    def inc(ins, e, n=1):
+        ins.then_inc(e["s"], n)
+        e["n"] += n
+
+    def need(q, *es):
+        for e in es:
+            if waited.get((q, e["k"]), 0) < e["n"]:
+                Q[q].wait_ge(e["s"], e["n"])
+                waited[(q, e["k"])] = e["n"]
+
+    def ts(e, out, in0, s1, s2, op0, op1=None):
+        if op1 is None:
+            inc(v.tensor_scalar(out, in0, s1, None, op0), e)
+        else:
+            inc(v.tensor_scalar(out, in0, s1, s2, op0, op1), e)
+
+    def tt(e, out, in0, in1, op):
+        inc(v.tensor_tensor(out, in0, in1, op), e)
+
+    def cp(e, out, in_):
+        inc(v.tensor_copy(out, in_), e)
+
+    def rnd(e, out, in0, unit):
+        inc(v.tensor_scalar(out, in0, RND * unit, -RND * unit, OP.add, OP.add), e)
+
+    def scan(e, out, resets, in_):
+        inc(v.tensor_tensor_scan(out, resets, in_, 0.0, OP.mult, OP.add), e)
+
+    def bits(m):
+        return [b for b in range(16) if (m >> b) & 1]
+
+    def plan(dsts):
+        out = {}
+        off = [d for d in dsts if topo.chip(d) != topo.chip(core)]
+        on = [d for d in dsts if topo.chip(d) == topo.chip(core)]
+        ob = bits(topo.mask(core, off[0]))
+        per = 1
+        while per * 2 * len(off) <= len(ob):
+            per *= 2
+        for i, d in enumerate(off):
+            out[d] = ob[i * per:(i + 1) * per]
+        for d in on:
+            out[d] = [b for b in bits(topo.mask(core, d)) if b not in ob][:2]
+        return out
+
+    def send(srv, me, src, dst, w, rsem):
+        e = ev()
+        pl = plan([c for c in srv if c != core])
+        tr = []
+        for i, d in enumerate(srv):
+            if d == core:
+                continue
+            rid, pid, _ = topo.addr(d)
+            tr.append(RemoteDMATransfer(dst_ids=[DstId(rid=rid, pnc=pid)], dma_engine_mask=sum(1 << b for b in pl[d]),
+                                        remote_sem=rsem, src=src[:, i * w:(i + 1) * w], dst=dst[:, me * w:(me + 1) * w]))
+            e["n"] += len(pl[d])
+        g.remote_dma_fused(tr, local_sem=e["s"])
+        return e
+
+    def arrivals(srv, rsem):
+        e = ev(rsem)
+        pl = plan([c for c in srv if c != core])
+        e["n"] = sum(len(b) for b in pl.values())
+        return e
+
+    aArr, bArr = arrivals(sM, T.sem.aArr), arrivals(sM, T.sem.bArr)
+    cArr, dArr = arrivals(sT, T.sem.cArr), arrivals(sT, T.sem.dArr)
+    full = topo.mask(core, partner)
+    nfull = len(bits(full))
+    prid, ppid, _ = topo.addr(partner)
+
+    def exchange(buf, a, b, rsem, e):
+        g.remote_dma(buf[:, a:b], buf[:, a:b], rsem, e["s"], ppid, prid, full)
+        e["n"] += nfull
+
+    eIx = ev()
+    inc(sy.dma_start(T.ix[:], T.idx[:]), eIx, 16)
+    m0 = 2049 * part if LANE_M else 0
+    eM = []
+    for h in range(MC):
+        eM.append(ev())
+        inc(sy.dma_start(T.winM[:, m0 + h * MW:m0 + (h + 1) * MW], T.mp[:, h * 8 * MW:(h + 1) * 8 * MW]), eM[h], 16)
+
+    def iota(out, pattern, base, cm):
+        e = ev()
+        inc(g.iota(out, pattern, base, cm, allow_small_or_imprecise_dtypes=True), e)
+        return e
+    iJK = iota(A("JK"), [[1, 128]], 0, -1)
+    iI16 = iota(A("I16"), [[0, 10], [1, 16]], 0, 0)
+    iREP = iota(A("REP"), [[1, 4]], 0, 0)
+    iI128 = iota(A("I128"), [[1, 128]], 0, 0)
+    iN16 = iota(A("N16"), [[16, 80]], 0, 0)
+
+    eC1 = ev()
+    eZ = ev()
+    inc(v.memset(A("ones"), 1.0), eC1)
+    inc(v.memset(T.zero[:], 0), eZ)
+    need("a", eZ)
+    eZd = ev()
+    inc(sc.dma_start(T.winM[:, 2048:2049], T.zero[:, 0:1]), eZd, 16)
+    need("v", iJK)
+    eL = ev()
+    ts(eL, A("Lt"), A("JK"), 0.0, -7.5, OP.is_equal, OP.mult)
+    ts(eL, A("Lu"), A("JK"), 0.0, None, OP.is_gt)
+    need("v", eL)
+    tt(eC1, A("Lp"), A("Lt"), A("Lu"), OP.add)
+    need("v", iI16)
+    ts(eC1, T.row[0:1, 0:64], T.pb[0:1, 0:64], float(szM), None, OP.mult)
+    ts(eC1, A("rst"), A("I16"), 0.0, None, OP.is_gt)
+    need("v", iREP)
+    cp(eC1, T.rep[:], A("REP"))
+
+    def rank_bias(a):
+        e = ev()
+        o = PLACE["ones"][1]
+        inc(pe.matmul(T.b0[:, 0:64], T.pb[0:1, o:o + 128], T.row[0:1, a:a + 64], True, False), e)
+        return e
+
+    def rank_mm(E, e):
+        inc(pe.matmul(T.b0[:, 0:64], A("Lp"), A(E), False, False), e)
+        for d in (1, 2, 3):
+            inc(pe.matmul(T.b0[:, 16 * d:64], A("ones"), A(E, 0, 64 - 16 * d), False, d == 3), e)
+
+    need("p", eC1)
+    eRA = rank_bias(0)
+
+    need("v", eIx, eC1)
+    e1 = ev()
+    ts(e1, A("bI"), T.ix[:], 19 if LANE_M else 18, None, SR)
+    need("v", e1)
+    eEA = ev()
+    tt(eEA, A("EA"), A("bI").indirect(T.rep[:, 0:4]), A("I16", 0, 64), OP.is_equal)
+    need("p", eEA)
+    rank_mm("EA", eRA)
+    e2 = ev()
+    if LANE_M:
+        ts(e2, A("iPart"), T.ix[:], 18, 1, SR, AND)
+    ts(e2, A("iCl"), T.ix[:], 4, MW - 1, SR, AND)
+    ts(e2, A("iCh"), T.ix[:], 7, 2048 - MW, SR, AND)
+    ts(e2, A("iG"), T.ix[:], 1, 7, SR, AND)
+    need("v", e2)
+    e3 = ev()
+    if LANE_M:
+        ts(e3, A("dP"), A("iPart"), 2049.0, -2048.0, OP.mult, OP.add)
+    else:
+        ts(e3, A("dP"), A("iG"), 0.0, -2048.0, OP.mult, OP.add)
+    tt(e3, A("dC"), A("iCl"), A("iCh"), OP.add)
+    ts(e3, A("g16"), A("iG"), 16.0, 7.5, OP.mult, OP.add)
+    need("v", e3)
+    e4 = ev()
+    tt(e4, A("delta"), A("dC"), A("dP"), OP.add)
+
+    def slots(E, R, S, c16, h, eR):
+        need("v", eR)
+        a, b, c, d = ev(), ev(), ev(), ev()
+        tt(a, A(R), T.b0[:, 0:64], A(E), OP.mult)
+        need("v", a)
+        scan(b, A(S), A("rst", 0, 64), A(R))
+        need("v", b)
+        rnd(c, A(c16), A(S, 15, 64, 16), 16)
+        need("v", c)
+        tt(d, A(h), A(S, 15, 64, 16), A(c16), OP.subtract)
+        need("v", d)
+
+    slots("EA", "RA", "SA", "c16A", "hA", eRA)
+    e5 = ev()
+    tt(e5, A("mcol"), A("hA"), A("g16"), OP.add)
+    need("v", e5, e4, iI128, iN16)
+    eSA = ev()
+    for k in range(4):
+        b = ev()
+        l, r = T.lA[:, 128 * k:128 * k + 128], T.rA[:, 80 * k:80 * k + 80]
+        ts(b, l, A("I128"), A("mcol", k, k + 1), None, OP.is_equal)
+        ts(b, r, A("N16"), A("c16A", k, k + 1), A("delta", k, k + 1), OP.is_equal, OP.mult)
+        need("p", b)
+        inc(pe.matmul(T.b1[:, 0:80], l, r, k == 0, k == 3), eSA)
+    need("v", eSA)
+    eA1 = ev()
+    eA2 = ev()
+    wM, wT = szM // 16, szT // 16
+    ts(eA1, T.sendA[:], T.b1[:, 0:80], 2048.0, None, OP.add)
+    ts(eA2, T.offA[:, wM * meM:wM * meM + wM], T.b1[:, wM * meM:wM * meM + wM], 2048.0, None, OP.add)
+
+    eMx = ev()
+    if LANE_M:
+        need("g", eM[0])
+        exchange(T.winM, m0, m0 + MW, T.sem.mArr, eMx)
+    need("g", eA1)
+    locA = send(sM, meM, T.sendA, T.offA, wM, T.sem.aArr)
+    if LANE_M:
+        need("g", *eM)
+        exchange(T.winM, m0 + MW, m0 + 2048, T.sem.mArr, eMx)
+
+    t0 = 8192 * part if LANE_T else 0
+    eT = [ev(), ev()]
+    need("y", locA)
+    if LANE_M:
+        need("y", eMx)
+    inc(sy.dma_start(T.winT[:, t0:t0 + 4096], T.tab[:, 0:4096]), eT[0], 16)
+
+    iPI = iota(A("PI"), [[0, 2]], 0, 1)
+    iI160 = iota(A("I160"), [[1, 160]], 0, 0)
+    iTC = iota(A("TC"), [[0, 4], [NT, 16]], 0, 0)
+    i32r = iota(A("I32r"), [[0, 4], [1, 32]], 0, 0)
+    iZ4 = iota(A("Z4"), [[1, 8], [0, 4]], 0, 0)
+
+    f1, f2, f3, f4, f5 = ev(), ev(), ev(), ev(), ev()
+    ts(f1, A("a0"), A("SA", 15, 64, 16), -56.0, None, OP.add)
+    ts(f1, A("iNl"), T.ix[:], 1, None, AND)
+    ts(f1, A("iNh"), T.ix[:], {4: 13, 2: 14}[MC], 7, SR, AND)
+    need("v", f1)
+    rnd(f2, A("u128"), A("a0"), 128)
+    ts(f2, A("n1"), A("iNl"), 8.0, None, OP.mult)
+    need("v", f2)
+    tt(f3, A("pl0"), A("a0"), A("u128"), OP.subtract)
+    tt(f3, A("n2"), A("n1"), A("iNh"), OP.add)
+    ts(f3, A("u8"), A("u128"), 0.125, None, OP.mult)
+    need("v", f3)
+    ts(f4, A("pl"), A("pl0"), 63.5, None, OP.add)
+    tt(f4, A("qc"), A("n2"), A("u8"), OP.add)
+    need("v", f4, iI160, iPI)
+    for k in range(4):
+        ts(f5, T.lQ[:, 128 * k:128 * k + 128], A("I128"), A("pl", k, k + 1), None, OP.is_equal)
+        ts(f5, T.rQ[:, 160 * k:160 * k + 160], A("I160"), A("qc", k, k + 1), None, OP.is_equal)
+    k1, k2, kS = ev(), ev(), ev()
+    ts(k1, A("P15"), A("PI", 0, 1), 15, None, AND)
+    ts(k1, A("P7"), A("PI", 0, 1), 7, None, AND)
+    ts(k1, A("PS3"), A("PI", 0, 1), 3, None, SR)
+    ts(k1, A("P3"), A("PI"), 3, None, AND)
+    ts(k1, A("ident"), A("JK"), 0.0, None, OP.is_equal)
+    ts(k1, A("U128"), A("I16", 0, 32), 128.0, None, OP.mult)
+    need("v", k1)
+    cp(k2, A("PF", 0, 1), A("P15"))
+    cp(k2, A("PF", 1, 2), A("P7"))
+    cp(k2, A("PF", 2, 3), A("PS3"))
+    need("v", k2)
+    ts(kS, A("S16"), A("I16", 0, 16), A("PF", 0, 1), None, OP.is_equal)
+    need("p", f5, k1)
+    eQ, eTr, eTk = ev(), ev(), ev()
+    for k in range(4):
+        inc(pe.matmul(T.b2[:, 0:160], T.lQ[:, 128 * k:128 * k + 128], T.rQ[:, 160 * k:160 * k + 160], k == 0, k == 3), eQ)
+    for k in range(4):
+        inc(pe.transpose(T.b6[:, 128 * k:128 * k + 128], T.lQ[:, 128 * k:128 * k + 128], A("ident")), eTr)
+    need("a", eTr)
+    inc(sc.activation(T.Tk[:], T.b6[:, 0:512], COPY), eTk)
+
+    if LANE_M:
+        eMa = ev(T.sem.mArr)
+        eMa["n"] = 2 * nfull
+        need("v", eMa)
+    need("v", aArr, eA1, eA2, eZd, *eM)
+    eGm = [ev(), ev()]
+    need("p", kS)
+    for q in range(5):
+        e = ev()
+        cp(e, T.G[:, 256 * q:256 * q + 256], T.winM[:, 0:NM].indirect(T.offA[:, 16 * q:16 * q + 16]))
+        need("p", e)
+        bank, o = (T.b3, 0) if q < 3 else (T.b4, 96)
+        for u in (2 * q, 2 * q + 1):
+            inc(pe.matmul(bank[:, 16 * u - o:16 * u - o + 16], T.G[:, 128 * u:128 * u + 128], A("S16"), True, True), eGm[0 if q < 3 else 1])
+    eB1, eB2, eB3 = ev(), ev(), ev()
+    need("a", eGm[0])
+    inc(sc.activation(T.sendB[:, 0:96], T.b3[:, 0:96], COPY), eB1)
+    need("v", eGm[1])
+    cp(eB3, T.sendB[:, 96:160], T.b4[:, 0:64])
+    need("g", eB1, eB3)
+    bw = 16 * (szM // 128)
+    locB = send(sM, meM, T.sendB, T.landB, bw, T.sem.bArr)
+    need("v", eB1, eB3)
+    cp(eB2, T.landB[:, bw * meM:bw * meM + bw], T.sendB[:, bw * meM:bw * meM + bw])
+
+    need("y", locB)
+    inc(sy.dma_start(T.winT[:, t0 + 4096:t0 + 8192], T.tab[:, 4096:8192]), eT[1], 16)
+    eTx = ev()
+    if LANE_T:
+        need("g", eT[0])
+        exchange(T.winT, t0, t0 + 4096, T.sem.tArr, eTx)
+        need("g", eT[1])
+        exchange(T.winT, t0 + 4096, t0 + 8192, T.sem.tArr, eTx)
+
+    need("v", iTC, i32r, iZ4)
+    k3, k3r = ev(), ev()
+    for k in range(4):
+        ts(k3, A("mask2", 32 * k, 32 * k + 32), A("U128"), A("u128", k, k + 1), None, OP.is_equal)
+    inc(v.memset(A("HL"), 0.0), k3)
+    inc(v.memset(T.row[0:1, 128:256], -NT / 2.0), k3r)
+    need("v", k3r)
+    for k in range(4):
+        inc(v.memset(T.row[0:1, 144 + 32 * k:160 + 32 * k], 0.5), k3)
+    ts(k3, A("rst32"), A("I32r"), 0.0, None, OP.is_gt)
+    ts(k3, T.row[0:1, 64:128], T.pb[0:1, 0:64], float(szT), None, OP.mult)
+    ts(k3, A("I16m"), A("I16", 0, 128), -7.5, None, OP.add)
+    cp(k3, T.repF[:], A("P3"))
+    ts(k3, T.lF[:], A("I16", 0, 128), A("PF", 2, 3), None, OP.is_equal)
+    ts(k3, A("Z0"), A("Z4"), A("PF", 1, 2), None, OP.is_equal)
+    need("v", k3)
+    need("p", k3)
+    eDm = ev()
+    o1 = PLACE["ones"][1]
+    inc(pe.matmul(T.b5[:, 0:128], T.pb[0:1, o1:o1 + 128], T.row[0:1, 128:256], True, False), eDm)
+    eRC = rank_bias(64)
+
+    need("v", bArr, eB2, eQ)
+    x1, x2, x3, x4, x5, x6, x7, x8, x9, x10 = [ev() for _ in range(10)]
+    tt(x1, A("X"), T.landB[:], T.b2[:, 0:160], OP.mult)
+    need("v", x1)
+    scan(x2, A("SX"), A("rst"), A("X"))
+    need("v", x2)
+    rnd(x3, A("HL", 0, 10), A("SX", 15, 160, 16), 512)
+    need("v", x3)
+    tt(x4, A("HL", 16, 26), A("SX", 15, 160, 16), A("HL", 0, 10), OP.subtract)
+    need("p", x3, x4, eTk)
+    for k in range(4):
+        inc(pe.matmul(T.b5[:, 32 * k:32 * k + 32], T.Tk[:, 128 * k:128 * k + 128], A("HL"), False, k == 3), eDm)
+    need("v", eDm)
+    tt(x5, A("D1"), T.b5[:, 0:128], A("mask2"), OP.mult)
+    need("v", x5)
+    scan(x6, A("SD"), A("rst32"), A("D1"))
+    need("v", x6)
+    rnd(x7, A("tU"), A("SD", 31, 128, 32), NT)
+    need("v", x7)
+    eEC = ev()
+    tt(eEC, A("EC"), A("tU").indirect(T.rep[:, 0:4]), A("TC"), OP.is_equal)
+    need("p", eEC)
+    rank_mm("EC", eRC)
+    tt(x8, A("lc"), A("SD", 31, 128, 32), A("tU"), OP.subtract)
+    need("v", x8)
+    rnd(x9, A("hi2"), A("lc"), 64)
+    need("v", x9)
+    tt(x10, A("lo2"), A("lc"), A("hi2"), OP.subtract)
+    slots("EC", "RC", "SC", "c16C", "sC", eRC)
+    need("v", x10)
+    eSC = ev()
+    for k in range(4):
+        b = ev()
+        l, r = T.lC[:, 128 * k:128 * k + 128], [T.rC[:, 160 * k + 80 * q:160 * k + 80 * q + 80] for q in (0, 1)]
+        ts(b, l, A("I16m"), A("sC", k, k + 1), None, OP.is_equal)
+        ts(b, r[0], A("N16"), A("c16C", k, k + 1), A("hi2", k, k + 1), OP.is_equal, OP.mult)
+        ts(b, r[1], A("N16"), A("c16C", k, k + 1), A("lo2", k, k + 1), OP.is_equal, OP.mult)
+        need("p", b)
+        for q in (0, 1):
+            inc(pe.matmul(T.b1[:, 0:80], l, r[q], k == 0 and q == 0, k == 3 and q == 1), eSC)
+    need("v", eSC)
+    eCs1, eCs2 = ev(), ev()
+    ts(eCs1, T.sendC[:], T.b1[:, 0:80], NT / 2 - 0.5, None, OP.add)
+    ts(eCs2, T.offC[:, wT * meT:wT * meT + wT], T.b1[:, wT * meT:wT * meT + wT], NT / 2 - 0.5, None, OP.add)
+    need("g", eCs1)
+    locC = send(sT, meT, T.sendC, T.offC, wT, T.sem.cArr)
+
+    y1, y2, y3, y4 = ev(), ev(), ev(), ev()
+    ts(y1, A("slotC"), A("SC", 15, 64, 16), 7.5, None, OP.add)
+    need("v", y1)
+    tt(y2, T.rF[:], A("slotC").indirect(T.repF[:, 0:2]), A("Z0"), OP.mult)
+    need("p", y2)
+    inc(pe.matmul(T.b7[:, 0:32], T.lF[:], T.rF[:], True, True), y3)
+    need("v", y3)
+    cp(y4, T.offF[:], T.b7[:, 0:32])
+
+    eD1, eD2, eD3 = ev(), ev(), ev()
+    if LANE_T:
+        eTa = ev(T.sem.tArr)
+        eTa["n"] = 2 * nfull
+        need("v", eTa)
+        need("a", eTa)
+    for q in ("v", "a"):
+        need(q, cArr, eCs2, eT[0], eT[1])
+    cp(eD1, T.sendD[:, 0:640], T.winT[:, 0:NT].indirect(T.offC[:, 0:40]))
+    inc(sc.activation(T.sendD[:, 640:1280], T.winT[:, 0:NT].indirect(T.offC[:, 40:80]), COPY), eD3)
+    need("g", eD1, eD3)
+    locD = send(sT, meT, T.sendD, T.landD, szT, T.sem.dArr)
+    need("v", eD1, eD3)
+    cp(eD2, T.landD[:, szT * meT:szT * meT + szT], T.sendD[:, szT * meT:szT * meT + szT])
+
+    for q in ("v", "a"):
+        need(q, dArr, eD2, y4)
+    eY1, eY2, eS1, eS2 = ev(), ev(), ev(), ev()
+    cp(eY1, T.yo[:, 0:256], T.landD[:, 0:1280].indirect(T.offF[:, 0:16]))
+    inc(sc.activation(T.yo[:, 256:512], T.landD[:, 0:1280].indirect(T.offF[:, 16:32]), COPY), eY2)
+    need("y", eY1)
+    inc(sy.dma_start(T.y[:, 0:256], T.yo[:, 0:256]), eS1, 16)
+    need("a", eY2)
+    inc(sc.dma_start(T.y[:, 256:512], T.yo[:, 256:512]), eS2, 16)
+    need("y", eS1)
+    need("a", eS2)
+    done = set(k for (_, k), n in waited.items() if n == groups[k]["n"])
+    for e in groups:
+        if e["n"] > 0 and e["k"] not in done:
+            need("g", e)

@@ -2,12 +2,11 @@ import numpy as np
 from concourse.bass import DstId, RemoteDMATransfer
 from concourse.mybir import dt, AluOpType, ActivationFunctionType
 
-LANE_M = True
-LANE_T = True
 MC = 4
 MW = 2048 // MC
-NM = 4097 if LANE_M else 2049
-NT = 16384 if LANE_T else 8192
+NM = 4097
+NT = 16384
+SZ, W = 256, 16
 NEV = 140
 F32, BF, FP, I32, U16 = "float32", "bfloat16", "float16", "int32", "uint16"
 
@@ -23,19 +22,19 @@ SCRATCH = {
     "lQ": _sb(512, BF), "rQ": _sb(640, BF), "Tk": _sb(512, BF), "lC": _sb(512, BF), "rC": _sb(640, BF),
     "rep": _sb(4, U16), "repF": _sb(2, U16), "offF": _sb(32, U16),
     "sendA": _sb(80, U16), "offA": _sb(80, U16), "sendC": _sb(80, U16), "offC": _sb(80, U16),
-    "G": _sb(1280, F32), "sendB": _sb(160, F32), "landB": _sb(160, F32),
+    "G": _sb(1280, F32), "sendB": _sb(128, F32), "landB": _sb(160, F32),
     "sendD": _sb(1280, BF), "landD": _sb(1280, BF), "yo": _sb(512, BF),
 }
 PACK = {
-    ("pf", F32): [("dP", 4), ("dC", 4), ("delta", 4), ("g16", 4), ("c16A", 4), ("hA", 4), ("mcol", 4), ("a0", 4), ("u128", 4),
-                  ("u8", 4), ("pl0", 4), ("pl", 4), ("n1", 4), ("n2", 4), ("qc", 4), ("tU", 4), ("lc", 4), ("hi2", 4), ("lo2", 4),
+    ("pf", F32): [("dP", 4), ("dC", 4), ("delta", 4), ("c16A", 4), ("hA", 4), ("mcol", 4), ("a0", 4), ("u16", 4),
+                  ("pl", 4), ("n1", 4), ("n2", 4), ("qc", 4), ("tU", 4), ("lc", 4), ("hi2", 4), ("lo2", 4),
                   ("c16C", 4), ("sC", 4), ("slotC", 4), ("PF", 4), ("S16", 16), ("Z0", 32), ("RA", 64), ("SA", 64), ("RC", 64),
                   ("SC", 64), ("X", 160), ("SX", 160), ("D1", 128), ("SD", 128), ("mask2", 128)],
     ("pi", I32): [("bI", 4), ("iPart", 4), ("iCl", 4), ("iCh", 4), ("iG", 4), ("iNl", 4), ("iNh", 4), ("REP", 4), ("PI", 2),
                   ("P3", 2), ("P15", 1), ("P7", 1), ("PS3", 1)],
-    ("pb", BF): [("I16", 160), ("I128", 128), ("JK", 128), ("N16", 80), ("I160", 160), ("TC", 64), ("I32r", 128), ("Z4", 32),
+    ("pb", BF): [("I16", 160), ("I128", 128), ("JK", 128), ("N2", 80), ("I160", 160), ("TC", 64), ("I32r", 128), ("Z4", 32),
                  ("ones", 128), ("Lt", 128), ("Lu", 128), ("Lp", 128), ("ident", 128), ("rst", 160), ("rst32", 128),
-                 ("I16m", 128), ("U128", 32), ("EA", 64), ("EC", 64), ("HL", 32)],
+                 ("I16m", 128), ("I128m", 128), ("I128q", 128), ("U16", 32), ("EA", 64), ("EC", 64), ("HL", 32)],
 }
 PLACE = {}
 for (_b, _d), _l in PACK.items():
@@ -68,25 +67,20 @@ def rank_program(g, core, T, topo):
             chips.append(topo.chip(c))
     partner = [c for c in cores if c != core and topo.chip(c) == topo.chip(core)][0]
     part = rank % 2
+    lane = [[c for c in cores if topo.chip(c) == ch and topo.die(c) == topo.die(core)][0] for ch in chips]
+    nl, me = len(lane), lane.index(core)
+    order = [(me + d) % nl for d in range(1, nl)]
+    phases = [order[0:2], order[2:4]]
 
     def A(name, a=0, b=None, step=1):
         buf, o, w = PLACE[name]
         b = w if b is None else b
         return T[buf][:, o + a:o + b:step] if step > 1 else T[buf][:, o + a:o + b]
 
-    def servers(lane):
-        if not lane:
-            return list(cores)
-        return [[c for c in cores if topo.chip(c) == ch and topo.die(c) == topo.die(core)][0] for ch in chips]
-
-    sM, sT = servers(LANE_M), servers(LANE_T)
-    meM, meT = sM.index(core), sT.index(core)
-    szM, szT = 1280 // len(sM), 1280 // len(sT)
-
     groups, waited = [], {}
 
-    def ev(sem=None):
-        e = {"s": sem if sem is not None else T.sem["e%d" % len(groups)], "n": 0, "k": len(groups)}
+    def ev(sem=None, n=0):
+        e = {"s": sem if sem is not None else T.sem["e%d" % len(groups)], "n": n, "k": len(groups)}
         groups.append(e)
         return e
 
@@ -112,6 +106,9 @@ def rank_program(g, core, T, topo):
     def cp(e, out, in_):
         inc(v.tensor_copy(out, in_), e)
 
+    def acp(e, out, in_):
+        inc(sc.activation(out, in_, COPY), e)
+
     def rnd(e, out, in0, unit):
         inc(v.tensor_scalar(out, in0, RND * unit, -RND * unit, OP.add, OP.add), e)
 
@@ -121,53 +118,35 @@ def rank_program(g, core, T, topo):
     def bits(m):
         return [b for b in range(16) if (m >> b) & 1]
 
-    def plan(dsts):
-        out = {}
-        off = [d for d in dsts if topo.chip(d) != topo.chip(core)]
-        on = [d for d in dsts if topo.chip(d) == topo.chip(core)]
-        ob = bits(topo.mask(core, off[0]))
-        per = 1
-        while per * 2 * len(off) <= len(ob):
-            per *= 2
-        for i, d in enumerate(off):
-            out[d] = ob[i * per:(i + 1) * per]
-        for d in on:
-            out[d] = [b for b in bits(topo.mask(core, d)) if b not in ob][:2]
-        return out
-
-    def send(srv, me, src, dst, w, rsem):
+    def send(members, src, at, dst, w, rsem):
         e = ev()
-        pl = plan([c for c in srv if c != core])
+        ob = bits(topo.mask(core, lane[members[0]]))
+        per = len(ob) // len(members)
         tr = []
-        for i, d in enumerate(srv):
-            if d == core:
-                continue
-            rid, pid, _ = topo.addr(d)
-            tr.append(RemoteDMATransfer(dst_ids=[DstId(rid=rid, pnc=pid)], dma_engine_mask=sum(1 << b for b in pl[d]),
-                                        remote_sem=rsem, src=src[:, i * w:(i + 1) * w], dst=dst[:, me * w:(me + 1) * w]))
-            e["n"] += len(pl[d])
+        for n, (i, s) in enumerate(zip(members, at)):
+            rid, pid, _ = topo.addr(lane[i])
+            tr.append(RemoteDMATransfer(dst_ids=[DstId(rid=rid, pnc=pid)], dma_engine_mask=sum(1 << b for b in ob[n * per:(n + 1) * per]),
+                                        remote_sem=rsem, src=src[:, s * w:(s + 1) * w], dst=dst[:, me * w:(me + 1) * w]))
+            e["n"] += per
         g.remote_dma_fused(tr, local_sem=e["s"])
         return e
 
-    def arrivals(srv, rsem):
-        e = ev(rsem)
-        pl = plan([c for c in srv if c != core])
-        e["n"] = sum(len(b) for b in pl.values())
-        return e
-
-    aArr, bArr = arrivals(sM, T.sem.aArr), arrivals(sM, T.sem.bArr)
-    cArr, dArr = arrivals(sT, T.sem.cArr), arrivals(sT, T.sem.dArr)
+    leave = topo.mask(core, lane[order[0]])
+    noff = len(bits(leave))
+    aArr, cArr = ev(T.sem.aArr, noff), ev(T.sem.cArr, noff)
+    bArr, dArr = ev(T.sem.bArr, 2 * noff), ev(T.sem.dArr, 2 * noff)
     full = topo.mask(core, partner)
-    nfull = len(bits(full))
+    stay = full & ~leave
+    nfull, nstay = len(bits(full)), len(bits(stay))
     prid, ppid, _ = topo.addr(partner)
 
-    def exchange(buf, a, b, rsem, e):
-        g.remote_dma(buf[:, a:b], buf[:, a:b], rsem, e["s"], ppid, prid, full)
-        e["n"] += nfull
+    def exchange(buf, a, b, rsem, e, mask):
+        g.remote_dma(buf[:, a:b], buf[:, a:b], rsem, e["s"], ppid, prid, mask)
+        e["n"] += len(bits(mask))
 
     eIx = ev()
     inc(sy.dma_start(T.ix[:], T.idx[:]), eIx, 16)
-    m0 = 2049 * part if LANE_M else 0
+    m0 = 2049 * part
     eM = []
     for h in range(MC):
         eM.append(ev())
@@ -181,31 +160,31 @@ def rank_program(g, core, T, topo):
     iI16 = iota(A("I16"), [[0, 10], [1, 16]], 0, 0)
     iREP = iota(A("REP"), [[1, 4]], 0, 0)
     iI128 = iota(A("I128"), [[1, 128]], 0, 0)
-    iN16 = iota(A("N16"), [[16, 80]], 0, 0)
+    iN2 = iota(A("N2"), [[2, 80]], 0, 0)
 
-    eC1 = ev()
-    eZ = ev()
-    inc(v.memset(A("ones"), 1.0), eC1)
+    eC1, eC2, eZ, eZd, eL = ev(), ev(), ev(), ev(), ev()
+    inc(v.memset(A("ones"), 0.125), eC1)
     inc(v.memset(T.zero[:], 0), eZ)
     need("a", eZ)
-    eZd = ev()
     inc(sc.dma_start(T.winM[:, 2048:2049], T.zero[:, 0:1]), eZd, 16)
     need("v", iJK)
-    eL = ev()
-    ts(eL, A("Lt"), A("JK"), 0.0, -7.5, OP.is_equal, OP.mult)
-    ts(eL, A("Lu"), A("JK"), 0.0, None, OP.is_gt)
+    ts(eL, A("Lt"), A("JK"), 0.0, -0.9375, OP.is_equal, OP.mult)
+    ts(eL, A("Lu"), A("JK"), 0.0, 0.125, OP.is_gt, OP.mult)
     need("v", eL)
     tt(eC1, A("Lp"), A("Lt"), A("Lu"), OP.add)
     need("v", iI16)
-    ts(eC1, T.row[0:1, 0:64], T.pb[0:1, 0:64], float(szM), None, OP.mult)
+    ts(eC1, T.row[0:1, 0:64], T.pb[0:1, 0:64], float(SZ), None, OP.mult)
     ts(eC1, A("rst"), A("I16"), 0.0, None, OP.is_gt)
     need("v", iREP)
     cp(eC1, T.rep[:], A("REP"))
+    need("v", iI128)
+    ts(eC2, A("I128m"), A("I128"), -7.5, 0.125, OP.add, OP.mult)
 
-    def rank_bias(a):
+    o1 = PLACE["ones"][1]
+
+    def rank_bias():
         e = ev()
-        o = PLACE["ones"][1]
-        inc(pe.matmul(T.b0[:, 0:64], T.pb[0:1, o:o + 128], T.row[0:1, a:a + 64], True, False), e)
+        inc(pe.matmul(T.b0[:, 0:64], T.pb[0:1, o1:o1 + 128], T.row[0:1, 0:64], True, False), e)
         return e
 
     def rank_mm(E, e):
@@ -214,81 +193,76 @@ def rank_program(g, core, T, topo):
             inc(pe.matmul(T.b0[:, 16 * d:64], A("ones"), A(E, 0, 64 - 16 * d), False, d == 3), e)
 
     need("p", eC1)
-    eRA = rank_bias(0)
+    eRA = rank_bias()
 
     need("v", eIx, eC1)
-    e1 = ev()
-    ts(e1, A("bI"), T.ix[:], 19 if LANE_M else 18, None, SR)
+    e1, eEA, e2, e3, e4, e5, s1, s2, s3, s4 = [ev() for _ in range(10)]
+    ts(e1, A("bI"), T.ix[:], 19, None, SR)
     need("v", e1)
-    eEA = ev()
     tt(eEA, A("EA"), A("bI").indirect(T.rep[:, 0:4]), A("I16", 0, 64), OP.is_equal)
     need("p", eEA)
     rank_mm("EA", eRA)
-    e2 = ev()
-    if LANE_M:
-        ts(e2, A("iPart"), T.ix[:], 18, 1, SR, AND)
+    ts(e2, A("iPart"), T.ix[:], 18, 1, SR, AND)
     ts(e2, A("iCl"), T.ix[:], 4, MW - 1, SR, AND)
     ts(e2, A("iCh"), T.ix[:], 7, 2048 - MW, SR, AND)
-    ts(e2, A("iG"), T.ix[:], 1, 7, SR, AND)
+    ts(e2, A("iG"), T.ix[:], 14, None, AND)
+    need("v", eRA)
+    tt(s1, A("RA"), T.b0[:, 0:64], A("EA"), OP.mult)
     need("v", e2)
-    e3 = ev()
-    if LANE_M:
-        ts(e3, A("dP"), A("iPart"), 2049.0, -2048.0, OP.mult, OP.add)
-    else:
-        ts(e3, A("dP"), A("iG"), 0.0, -2048.0, OP.mult, OP.add)
+    ts(e3, A("dP"), A("iPart"), 2049.0, -2048.0, OP.mult, OP.add)
+    need("v", s1)
+    scan(s2, A("SA"), A("rst", 0, 64), A("RA"))
     tt(e3, A("dC"), A("iCl"), A("iCh"), OP.add)
-    ts(e3, A("g16"), A("iG"), 16.0, 7.5, OP.mult, OP.add)
+    need("v", s2)
+    rnd(s3, A("c16A"), A("SA", 15, 64, 16), 2)
     need("v", e3)
-    e4 = ev()
     tt(e4, A("delta"), A("dC"), A("dP"), OP.add)
+    need("v", s3)
+    tt(s4, A("hA"), A("SA", 15, 64, 16), A("c16A"), OP.subtract)
+    need("v", e4, iN2)
+    lb = [ev() for _ in range(4)]
 
-    def slots(E, R, S, c16, h, eR):
-        need("v", eR)
-        a, b, c, d = ev(), ev(), ev(), ev()
-        tt(a, A(R), T.b0[:, 0:64], A(E), OP.mult)
-        need("v", a)
-        scan(b, A(S), A("rst", 0, 64), A(R))
-        need("v", b)
-        rnd(c, A(c16), A(S, 15, 64, 16), 16)
-        need("v", c)
-        tt(d, A(h), A(S, 15, 64, 16), A(c16), OP.subtract)
-        need("v", d)
+    def rhsA(k):
+        ts(lb[k], T.rA[:, 80 * k:80 * k + 80], A("N2"), A("c16A", k, k + 1), A("delta", k, k + 1), OP.is_equal, OP.mult)
 
-    slots("EA", "RA", "SA", "c16A", "hA", eRA)
-    e5 = ev()
-    tt(e5, A("mcol"), A("hA"), A("g16"), OP.add)
-    need("v", e5, e4, iI128, iN16)
+    rhsA(0)
+    need("v", s4)
+    tt(e5, A("mcol"), A("hA"), A("iG"), OP.add)
+    rhsA(1)
+    need("v", e5, eC2)
     eSA = ev()
     for k in range(4):
-        b = ev()
+        if k > 1:
+            rhsA(k)
         l, r = T.lA[:, 128 * k:128 * k + 128], T.rA[:, 80 * k:80 * k + 80]
-        ts(b, l, A("I128"), A("mcol", k, k + 1), None, OP.is_equal)
-        ts(b, r, A("N16"), A("c16A", k, k + 1), A("delta", k, k + 1), OP.is_equal, OP.mult)
-        need("p", b)
+        ts(lb[k], l, A("I128m"), A("mcol", k, k + 1), None, OP.is_equal)
+        need("p", lb[k])
         inc(pe.matmul(T.b1[:, 0:80], l, r, k == 0, k == 3), eSA)
     need("v", eSA)
-    eA1 = ev()
-    eA2 = ev()
-    wM, wT = szM // 16, szT // 16
+    eA1, eA2 = ev(), ev()
     ts(eA1, T.sendA[:], T.b1[:, 0:80], 2048.0, None, OP.add)
-    ts(eA2, T.offA[:, wM * meM:wM * meM + wM], T.b1[:, wM * meM:wM * meM + wM], 2048.0, None, OP.add)
+    ts(eA2, T.offA[:, W * me:W * me + W], T.b1[:, W * me:W * me + W], 2048.0, None, OP.add)
 
     eMx = ev()
-    if LANE_M:
-        need("g", eM[0])
-        exchange(T.winM, m0, m0 + MW, T.sem.mArr, eMx)
+    for h, mask in ((0, full), (1, stay)):
+        need("g", eM[h])
+        exchange(T.winM, m0 + h * MW, m0 + (h + 1) * MW, T.sem.mArr, eMx, mask)
     need("g", eA1)
-    locA = send(sM, meM, T.sendA, T.offA, wM, T.sem.aArr)
-    if LANE_M:
-        need("g", *eM)
-        exchange(T.winM, m0 + MW, m0 + 2048, T.sem.mArr, eMx)
+    locA = send(order, T.sendA, order, T.offA, W, T.sem.aArr)
+    need("g", *eM)
+    exchange(T.winM, m0 + 2 * MW, m0 + 2048, T.sem.mArr, eMx, full)
 
-    t0 = 8192 * part if LANE_T else 0
-    eT = [ev(), ev()]
+    t0 = 8192 * part
+    eT = [ev(), ev(), ev(), ev()]
+
+    def load_table(q):
+        inc(sy.dma_start(T.winT[:, t0 + 2048 * q:t0 + 2048 * q + 2048], T.tab[:, 2048 * q:2048 * q + 2048]), eT[q], 16)
+
     need("y", locA)
-    if LANE_M:
-        need("y", eMx)
-    inc(sy.dma_start(T.winT[:, t0:t0 + 4096], T.tab[:, 0:4096]), eT[0], 16)
+    load_table(0)
+    load_table(1)
+    need("y", eT[0], eT[1])
+    load_table(2)
 
     iPI = iota(A("PI"), [[0, 2]], 0, 1)
     iI160 = iota(A("I160"), [[1, 160]], 0, 0)
@@ -297,22 +271,21 @@ def rank_program(g, core, T, topo):
     iZ4 = iota(A("Z4"), [[1, 8], [0, 4]], 0, 0)
 
     f1, f2, f3, f4, f5 = ev(), ev(), ev(), ev(), ev()
-    ts(f1, A("a0"), A("SA", 15, 64, 16), -56.0, None, OP.add)
+    ts(f1, A("a0"), A("SA", 15, 64, 16), -7.0, None, OP.add)
     ts(f1, A("iNl"), T.ix[:], 1, None, AND)
-    ts(f1, A("iNh"), T.ix[:], {4: 13, 2: 14}[MC], 7, SR, AND)
+    ts(f1, A("iNh"), T.ix[:], 13, 7, SR, AND)
+    ts(f1, A("I128q"), A("I128"), -63.5, 0.125, OP.add, OP.mult)
     need("v", f1)
-    rnd(f2, A("u128"), A("a0"), 128)
+    rnd(f2, A("u16"), A("a0"), 16)
     ts(f2, A("n1"), A("iNl"), 8.0, None, OP.mult)
     need("v", f2)
-    tt(f3, A("pl0"), A("a0"), A("u128"), OP.subtract)
+    tt(f3, A("pl"), A("a0"), A("u16"), OP.subtract)
     tt(f3, A("n2"), A("n1"), A("iNh"), OP.add)
-    ts(f3, A("u8"), A("u128"), 0.125, None, OP.mult)
     need("v", f3)
-    ts(f4, A("pl"), A("pl0"), 63.5, None, OP.add)
-    tt(f4, A("qc"), A("n2"), A("u8"), OP.add)
+    tt(f4, A("qc"), A("n2"), A("u16"), OP.add)
     need("v", f4, iI160, iPI)
     for k in range(4):
-        ts(f5, T.lQ[:, 128 * k:128 * k + 128], A("I128"), A("pl", k, k + 1), None, OP.is_equal)
+        ts(f5, T.lQ[:, 128 * k:128 * k + 128], A("I128q"), A("pl", k, k + 1), None, OP.is_equal)
         ts(f5, T.rQ[:, 160 * k:160 * k + 160], A("I160"), A("qc", k, k + 1), None, OP.is_equal)
     k1, k2, kS = ev(), ev(), ev()
     ts(k1, A("P15"), A("PI", 0, 1), 15, None, AND)
@@ -320,7 +293,7 @@ def rank_program(g, core, T, topo):
     ts(k1, A("PS3"), A("PI", 0, 1), 3, None, SR)
     ts(k1, A("P3"), A("PI"), 3, None, AND)
     ts(k1, A("ident"), A("JK"), 0.0, None, OP.is_equal)
-    ts(k1, A("U128"), A("I16", 0, 32), 128.0, None, OP.mult)
+    ts(k1, A("U16"), A("I16", 0, 32), 16.0, None, OP.mult)
     need("v", k1)
     cp(k2, A("PF", 0, 1), A("P15"))
     cp(k2, A("PF", 1, 2), A("P7"))
@@ -334,66 +307,59 @@ def rank_program(g, core, T, topo):
     for k in range(4):
         inc(pe.transpose(T.b6[:, 128 * k:128 * k + 128], T.lQ[:, 128 * k:128 * k + 128], A("ident")), eTr)
     need("a", eTr)
-    inc(sc.activation(T.Tk[:], T.b6[:, 0:512], COPY), eTk)
+    acp(eTk, T.Tk[:], T.b6[:, 0:512])
 
-    if LANE_M:
-        eMa = ev(T.sem.mArr)
-        eMa["n"] = 2 * nfull
-        need("v", eMa)
-    need("v", aArr, eA1, eA2, eZd, *eM)
-    eGm = [ev(), ev()]
+    eMa = ev(T.sem.mArr, 2 * nfull + nstay)
+    need("v", eMa, aArr, eA1, eA2, eZd, *eM)
     need("p", kS)
-    for q in range(5):
+    locB, eB2 = [], ev()
+    for p, (members, bank) in enumerate(((phases[0], T.b3), (phases[1], T.b4), ([me], T.b7))):
         e = ev()
-        cp(e, T.G[:, 256 * q:256 * q + 256], T.winM[:, 0:NM].indirect(T.offA[:, 16 * q:16 * q + 16]))
-        need("p", e)
-        bank, o = (T.b3, 0) if q < 3 else (T.b4, 96)
-        for u in (2 * q, 2 * q + 1):
-            inc(pe.matmul(bank[:, 16 * u - o:16 * u - o + 16], T.G[:, 128 * u:128 * u + 128], A("S16"), True, True), eGm[0 if q < 3 else 1])
-    eB1, eB2, eB3 = ev(), ev(), ev()
-    need("a", eGm[0])
-    inc(sc.activation(T.sendB[:, 0:96], T.b3[:, 0:96], COPY), eB1)
-    need("v", eGm[1])
-    cp(eB3, T.sendB[:, 96:160], T.b4[:, 0:64])
-    need("g", eB1, eB3)
-    bw = 16 * (szM // 128)
-    locB = send(sM, meM, T.sendB, T.landB, bw, T.sem.bArr)
-    need("v", eB1, eB3)
-    cp(eB2, T.landB[:, bw * meM:bw * meM + bw], T.sendB[:, bw * meM:bw * meM + bw])
+        for n, i in enumerate(members):
+            b = ev()
+            cp(b, T.G[:, SZ * i:SZ * i + SZ], T.winM[:, 0:NM].indirect(T.offA[:, W * i:W * i + W]))
+            need("p", b)
+            for u in (0, 1):
+                inc(pe.matmul(bank[:, 32 * n + 16 * u:32 * n + 16 * u + 16], T.G[:, SZ * i + 128 * u:SZ * i + 128 * u + 128], A("S16"), True, True), e)
+        if members == [me]:
+            need("v", e)
+            cp(eB2, T.landB[:, 32 * me:32 * me + 32], bank[:, 0:32])
+        else:
+            need("a", e)
+            c = ev()
+            acp(c, T.sendB[:, 64 * p:64 * p + 64], bank[:, 0:64])
+            need("g", c)
+            locB.append(send(members, T.sendB, [2 * p, 2 * p + 1], T.landB, 32, T.sem.bArr))
 
-    need("y", locB)
-    inc(sy.dma_start(T.winT[:, t0 + 4096:t0 + 8192], T.tab[:, 4096:8192]), eT[1], 16)
+    need("y", *locB)
+    load_table(3)
     eTx = ev()
-    if LANE_T:
-        need("g", eT[0])
-        exchange(T.winT, t0, t0 + 4096, T.sem.tArr, eTx)
-        need("g", eT[1])
-        exchange(T.winT, t0 + 4096, t0 + 8192, T.sem.tArr, eTx)
+    for q in range(4):
+        need("g", eT[q])
+        exchange(T.winT, t0 + 2048 * q, t0 + 2048 * q + 2048, T.sem.tArr, eTx, full)
 
     need("v", iTC, i32r, iZ4)
     k3, k3r = ev(), ev()
     for k in range(4):
-        ts(k3, A("mask2", 32 * k, 32 * k + 32), A("U128"), A("u128", k, k + 1), None, OP.is_equal)
+        ts(k3, A("mask2", 32 * k, 32 * k + 32), A("U16"), A("u16", k, k + 1), None, OP.is_equal)
     inc(v.memset(A("HL"), 0.0), k3)
-    inc(v.memset(T.row[0:1, 128:256], -NT / 2.0), k3r)
+    inc(v.memset(T.row[0:1, 128:256], -NT * 4.0), k3r)
     need("v", k3r)
     for k in range(4):
-        inc(v.memset(T.row[0:1, 144 + 32 * k:160 + 32 * k], 0.5), k3)
+        inc(v.memset(T.row[0:1, 144 + 32 * k:160 + 32 * k], 4.0), k3)
     ts(k3, A("rst32"), A("I32r"), 0.0, None, OP.is_gt)
-    ts(k3, T.row[0:1, 64:128], T.pb[0:1, 0:64], float(szT), None, OP.mult)
-    ts(k3, A("I16m"), A("I16", 0, 128), -7.5, None, OP.add)
+    ts(k3, A("I16m"), A("I16", 0, 128), -7.5, 0.125, OP.add, OP.mult)
     cp(k3, T.repF[:], A("P3"))
     ts(k3, T.lF[:], A("I16", 0, 128), A("PF", 2, 3), None, OP.is_equal)
     ts(k3, A("Z0"), A("Z4"), A("PF", 1, 2), None, OP.is_equal)
     need("v", k3)
     need("p", k3)
     eDm = ev()
-    o1 = PLACE["ones"][1]
     inc(pe.matmul(T.b5[:, 0:128], T.pb[0:1, o1:o1 + 128], T.row[0:1, 128:256], True, False), eDm)
-    eRC = rank_bias(64)
+    eRC = rank_bias()
 
     need("v", bArr, eB2, eQ)
-    x1, x2, x3, x4, x5, x6, x7, x8, x9, x10 = [ev() for _ in range(10)]
+    x1, x2, x3, x4, x5, x6, x7, x8, x9, x10, x11, x12 = [ev() for _ in range(12)]
     tt(x1, A("X"), T.landB[:], T.b2[:, 0:160], OP.mult)
     need("v", x1)
     scan(x2, A("SX"), A("rst"), A("X"))
@@ -418,29 +384,37 @@ def rank_program(g, core, T, topo):
     tt(x8, A("lc"), A("SD", 31, 128, 32), A("tU"), OP.subtract)
     need("v", x8)
     rnd(x9, A("hi2"), A("lc"), 64)
+    need("v", eRC)
+    tt(x11, A("RC"), T.b0[:, 0:64], A("EC"), OP.mult)
     need("v", x9)
     tt(x10, A("lo2"), A("lc"), A("hi2"), OP.subtract)
-    slots("EC", "RC", "SC", "c16C", "sC", eRC)
+    need("v", x11)
+    scan(x12, A("SC"), A("rst", 0, 64), A("RC"))
+    need("v", x12)
+    y1, y2, y3, y4, y5, y6 = ev(), ev(), ev(), ev(), ev(), ev()
+    rnd(y5, A("c16C"), A("SC", 15, 64, 16), 2)
+    need("v", y5)
+    tt(y6, A("sC"), A("SC", 15, 64, 16), A("c16C"), OP.subtract)
     need("v", x10)
     eSC = ev()
     for k in range(4):
         b = ev()
         l, r = T.lC[:, 128 * k:128 * k + 128], [T.rC[:, 160 * k + 80 * q:160 * k + 80 * q + 80] for q in (0, 1)]
+        ts(b, r[0], A("N2"), A("c16C", k, k + 1), A("hi2", k, k + 1), OP.is_equal, OP.mult)
+        ts(b, r[1], A("N2"), A("c16C", k, k + 1), A("lo2", k, k + 1), OP.is_equal, OP.mult)
+        need("v", y6)
         ts(b, l, A("I16m"), A("sC", k, k + 1), None, OP.is_equal)
-        ts(b, r[0], A("N16"), A("c16C", k, k + 1), A("hi2", k, k + 1), OP.is_equal, OP.mult)
-        ts(b, r[1], A("N16"), A("c16C", k, k + 1), A("lo2", k, k + 1), OP.is_equal, OP.mult)
         need("p", b)
         for q in (0, 1):
             inc(pe.matmul(T.b1[:, 0:80], l, r[q], k == 0 and q == 0, k == 3 and q == 1), eSC)
     need("v", eSC)
     eCs1, eCs2 = ev(), ev()
     ts(eCs1, T.sendC[:], T.b1[:, 0:80], NT / 2 - 0.5, None, OP.add)
-    ts(eCs2, T.offC[:, wT * meT:wT * meT + wT], T.b1[:, wT * meT:wT * meT + wT], NT / 2 - 0.5, None, OP.add)
+    ts(eCs2, T.offC[:, W * me:W * me + W], T.b1[:, W * me:W * me + W], NT / 2 - 0.5, None, OP.add)
     need("g", eCs1)
-    locC = send(sT, meT, T.sendC, T.offC, wT, T.sem.cArr)
+    locC = send(order, T.sendC, order, T.offC, W, T.sem.cArr)
 
-    y1, y2, y3, y4 = ev(), ev(), ev(), ev()
-    ts(y1, A("slotC"), A("SC", 15, 64, 16), 7.5, None, OP.add)
+    ts(y1, A("slotC"), A("SC", 15, 64, 16), 8.0, 7.5, OP.mult, OP.add)
     need("v", y1)
     tt(y2, T.rF[:], A("slotC").indirect(T.repF[:, 0:2]), A("Z0"), OP.mult)
     need("p", y2)
@@ -448,26 +422,26 @@ def rank_program(g, core, T, topo):
     need("v", y3)
     cp(y4, T.offF[:], T.b7[:, 0:32])
 
-    eD1, eD2, eD3 = ev(), ev(), ev()
-    if LANE_T:
-        eTa = ev(T.sem.tArr)
-        eTa["n"] = 2 * nfull
-        need("v", eTa)
-        need("a", eTa)
+    eTa = ev(T.sem.tArr, 4 * nfull)
     for q in ("v", "a"):
-        need(q, cArr, eCs2, eT[0], eT[1])
-    cp(eD1, T.sendD[:, 0:640], T.winT[:, 0:NT].indirect(T.offC[:, 0:40]))
-    inc(sc.activation(T.sendD[:, 640:1280], T.winT[:, 0:NT].indirect(T.offC[:, 40:80]), COPY), eD3)
-    need("g", eD1, eD3)
-    locD = send(sT, meT, T.sendD, T.landD, szT, T.sem.dArr)
-    need("v", eD1, eD3)
-    cp(eD2, T.landD[:, szT * meT:szT * meT + szT], T.sendD[:, szT * meT:szT * meT + szT])
+        need(q, eTa, cArr, eCs2, *eT)
+    for members in phases:
+        e = [ev(), ev()]
+        for n, i in enumerate(members):
+            src = T.winT[:, 0:NT].indirect(T.offC[:, W * i:W * i + W])
+            (cp, acp)[n](e[n], T.sendD[:, SZ * i:SZ * i + SZ], src)
+        need("g", *e)
+        send(members, T.sendD, members, T.landD, SZ, T.sem.dArr)
+    eD = [ev(), ev()]
+    for n in (0, 1):
+        a = SZ * me + 128 * n
+        (cp, acp)[n](eD[n], T.landD[:, a:a + 128], T.winT[:, 0:NT].indirect(T.offC[:, W * me + 8 * n:W * me + 8 * n + 8]))
 
     for q in ("v", "a"):
-        need(q, dArr, eD2, y4)
+        need(q, dArr, y4, *eD)
     eY1, eY2, eS1, eS2 = ev(), ev(), ev(), ev()
     cp(eY1, T.yo[:, 0:256], T.landD[:, 0:1280].indirect(T.offF[:, 0:16]))
-    inc(sc.activation(T.yo[:, 256:512], T.landD[:, 0:1280].indirect(T.offF[:, 16:32]), COPY), eY2)
+    acp(eY2, T.yo[:, 256:512], T.landD[:, 0:1280].indirect(T.offF[:, 16:32]))
     need("y", eY1)
     inc(sy.dma_start(T.y[:, 0:256], T.yo[:, 0:256]), eS1, 16)
     need("a", eY2)

@@ -7,7 +7,9 @@ MW = 2048 // MC
 NM = 4097
 NT = 16384
 SZ, W = 256, 16
-NEV = 140
+NEV = 142
+BIG = 512.0
+BIG2 = 262144.0
 F32, BF, FP, I32, U16 = "float32", "bfloat16", "float16", "int32", "uint16"
 
 
@@ -18,7 +20,7 @@ def _sb(n, d):
 SCRATCH = {
     "winM": _sb(NM + 3, I32), "winT": _sb(NT, BF), "zero": _sb(4, I32), "ix": _sb(4, I32),
     "row": _sb(256, BF),
-    "lA": _sb(512, FP), "rA": _sb(320, FP), "lF": _sb(128, FP), "rF": _sb(32, FP),
+    "lA": _sb(512, FP), "rA": _sb(320, FP), "N2h": _sb(80, FP), "lF": _sb(128, FP), "rF": _sb(32, FP),
     "lQ": _sb(512, BF), "rQ": _sb(640, BF), "Tk": _sb(512, BF), "lC": _sb(512, BF), "rC": _sb(640, BF),
     "rep": _sb(4, U16), "repF": _sb(2, U16), "offF": _sb(32, U16),
     "sendA": _sb(80, U16), "offA": _sb(80, U16), "sendC": _sb(80, U16), "offC": _sb(80, U16),
@@ -26,15 +28,16 @@ SCRATCH = {
     "sendD": _sb(1280, BF), "landD": _sb(1280, BF), "yo": _sb(512, BF),
 }
 PACK = {
-    ("pf", F32): [("dP", 4), ("dC", 4), ("delta", 4), ("c16A", 4), ("hA", 4), ("mcol", 4), ("a0", 4), ("u16", 4),
-                  ("pl", 4), ("n1", 4), ("n2", 4), ("qc", 4), ("tU", 4), ("lc", 4), ("hi2", 4), ("lo2", 4),
-                  ("c16C", 4), ("sC", 4), ("slotC", 4), ("PF", 4), ("S16", 16), ("Z0", 32), ("RA", 64), ("SA", 64), ("RC", 64),
-                  ("SC", 64), ("X", 160), ("SX", 160), ("D1", 128), ("SD", 128), ("mask2", 128)],
-    ("pi", I32): [("bI", 4), ("iPart", 4), ("iCl", 4), ("iCh", 4), ("iG", 4), ("iNl", 4), ("iNh", 4), ("REP", 4), ("PI", 2),
+    ("pf", F32): [("dP", 4), ("dC", 4), ("delta", 4), ("c16A", 4), ("mA", 4), ("a0", 4), ("u16", 4),
+                  ("pl", 4), ("n1", 4), ("n2", 4), ("qc", 4), ("tU", 4), ("lc", 4), ("hi2", 4), ("lo2", 4), ("lon", 4),
+                  ("c16C", 4), ("slotC", 4), ("PF", 4), ("S16", 16), ("Z0", 32), ("SA", 64), ("SC", 64),
+                  ("X", 160), ("SX", 160), ("SD", 64), ("N2f", 80)],
+    ("pi", I32): [("bI", 4), ("iPart", 4), ("iCl", 4), ("iCh", 4), ("iG", 4), ("iNl", 4), ("iNh", 4), ("PI", 2),
                   ("P3", 2), ("P15", 1), ("P7", 1), ("PS3", 1)],
-    ("pb", BF): [("I16", 160), ("I128", 128), ("JK", 128), ("N2", 80), ("I160", 160), ("TC", 64), ("I32r", 128), ("Z4", 32),
-                 ("ones", 128), ("Lt", 128), ("Lu", 128), ("Lp", 128), ("ident", 128), ("rst", 160), ("rst32", 128),
-                 ("I16m", 128), ("I128m", 128), ("I128q", 128), ("U16", 32), ("EA", 64), ("EC", 64), ("HL", 32)],
+    ("pb", BF): [("I16", 64), ("I16b", 160), ("I128", 128), ("JK", 128), ("I160", 160), ("TC", 64), ("Z4", 32),
+                 ("ones", 128), ("Lt", 128), ("Lu", 128), ("Lp", 128), ("ident", 128), ("rst64", 64), ("rst", 160),
+                 ("I16m", 128), ("I128m", 128), ("I128q", 128), ("U16", 16), ("EA", 64), ("EC", 64), ("HL", 32),
+                 ("mask2", 64), ("abQ", 256), ("abC", 160)],
 }
 PLACE = {}
 for (_b, _d), _l in PACK.items():
@@ -46,11 +49,11 @@ for (_b, _d), _l in PACK.items():
 for _k in (0, 1, 2, 3, 4, 5, 7):
     SCRATCH["b%d" % _k] = ("psum", [128, 512], F32)
 SCRATCH["b6"] = ("psum", [128, 1024], BF)
-SEMAPHORES = ["mArr", "aArr", "bArr", "tArr", "cArr", "dArr"] + ["e%d" % i for i in range(NEV)]
+SEMAPHORES = ["mArr", "aArr", "bArr0", "bArr1", "tArr", "cArr", "dArr"] + ["e%d" % i for i in range(NEV)]
 
 OP = AluOpType
 SR, AND = OP.logical_shift_right, OP.bitwise_and
-COPY = ActivationFunctionType.Copy
+FN = ActivationFunctionType
 RND = 1.5 * 2.0 ** 23
 
 
@@ -71,6 +74,7 @@ def rank_program(g, core, T, topo):
     nl, me = len(lane), lane.index(core)
     order = [(me + d) % nl for d in range(1, nl)]
     phases = [order[0:2], order[2:4]]
+    early = [me] + [(me - d) % nl for d in (1, 2)]
 
     def A(name, a=0, b=None, step=1):
         buf, o, w = PLACE[name]
@@ -106,14 +110,17 @@ def rank_program(g, core, T, topo):
     def cp(e, out, in_):
         inc(v.tensor_copy(out, in_), e)
 
-    def acp(e, out, in_):
-        inc(sc.activation(out, in_, COPY), e)
+    def fill(e, out, x):
+        inc(v.memset(out, x), e)
 
-    def rnd(e, out, in0, unit):
-        inc(v.tensor_scalar(out, in0, RND * unit, -RND * unit, OP.add, OP.add), e)
+    def act(e, out, in_, fn=FN.Copy, bias=0.0, scale=1.0):
+        inc(sc.activation(out, in_, fn, bias=bias, scale=scale), e)
 
-    def scan(e, out, resets, in_):
-        inc(v.tensor_tensor_scan(out, resets, in_, 0.0, OP.mult, OP.add), e)
+    def rnd(e, out, in0, unit, more=0.0):
+        inc(v.tensor_scalar(out, in0, RND * unit, more - RND * unit, OP.add, OP.add), e)
+
+    def scan(e, out, resets, in_, op):
+        inc(v.tensor_tensor_scan(out, resets, in_, 0.0, OP.mult, op), e)
 
     def bits(m):
         return [b for b in range(16) if (m >> b) & 1]
@@ -134,7 +141,8 @@ def rank_program(g, core, T, topo):
     leave = topo.mask(core, lane[order[0]])
     noff = len(bits(leave))
     aArr, cArr = ev(T.sem.aArr, noff), ev(T.sem.cArr, noff)
-    bArr, dArr = ev(T.sem.bArr, 2 * noff), ev(T.sem.dArr, 2 * noff)
+    bArr = [ev(T.sem.bArr0, noff), ev(T.sem.bArr1, noff)]
+    dArr = ev(T.sem.dArr, 3 * noff)
     full = topo.mask(core, partner)
     stay = full & ~leave
     nfull, nstay = len(bits(full)), len(bits(stay))
@@ -156,35 +164,38 @@ def rank_program(g, core, T, topo):
         e = ev()
         inc(g.iota(out, pattern, base, cm, allow_small_or_imprecise_dtypes=True), e)
         return e
+    iI16 = iota(A("I16"), [[0, 4], [1, 16]], 0, 0)
     iJK = iota(A("JK"), [[1, 128]], 0, -1)
-    iI16 = iota(A("I16"), [[0, 10], [1, 16]], 0, 0)
-    iREP = iota(A("REP"), [[1, 4]], 0, 0)
+    iN2 = iota(A("N2f"), [[2, 80]], int(BIG), 0)
     iI128 = iota(A("I128"), [[1, 128]], 0, 0)
-    iN2 = iota(A("N2"), [[2, 80]], 0, 0)
 
-    eC1, eC2, eZ, eZd, eL = ev(), ev(), ev(), ev(), ev()
-    inc(v.memset(A("ones"), 0.125), eC1)
-    inc(v.memset(T.zero[:], 0), eZ)
-    need("a", eZ)
-    inc(sc.dma_start(T.winM[:, 2048:2049], T.zero[:, 0:1]), eZd, 16)
+    o1, o16 = PLACE["ones"][1], PLACE["I16"][1]
+    eOne, eRep, eR0, eRow, eZ, eZd, eL, eLp, eN2 = [ev() for _ in range(9)]
+    eRst, eI128m, eI128q, eU16 = [ev() for _ in range(4)]
+    fill(eR0, T.row[0:2, 0:64], -7.5)
+    fill(eOne, A("ones"), 0.125)
+    for k in range(4):
+        fill(eRep, T.rep[:, k:k + 1], k)
+    need("v", iI16, eR0)
+    ts(eRow, T.row[0:1, 0:64], T.pb[0:1, o16:o16 + 64], float(SZ), None, OP.mult)
+    fill(eZ, T.zero[:], 0)
     need("v", iJK)
-    ts(eL, A("Lt"), A("JK"), 0.0, -0.9375, OP.is_equal, OP.mult)
+    ts(eL, A("Lt"), A("JK"), 0.0, BIG, OP.is_equal, OP.mult)
     ts(eL, A("Lu"), A("JK"), 0.0, 0.125, OP.is_gt, OP.mult)
     need("v", eL)
-    tt(eC1, A("Lp"), A("Lt"), A("Lu"), OP.add)
-    need("v", iI16)
-    ts(eC1, T.row[0:1, 0:64], T.pb[0:1, 0:64], float(SZ), None, OP.mult)
-    ts(eC1, A("rst"), A("I16"), 0.0, None, OP.is_gt)
-    need("v", iREP)
-    cp(eC1, T.rep[:], A("REP"))
-    need("v", iI128)
-    ts(eC2, A("I128m"), A("I128"), -7.5, 0.125, OP.add, OP.mult)
-
-    o1 = PLACE["ones"][1]
+    tt(eLp, A("Lp"), A("Lt"), A("Lu"), OP.add)
+    need("a", iI16)
+    act(eRst, A("rst64"), A("I16"), FN.Sign)
+    act(eU16, A("U16"), A("I16", 0, 16), scale=16.0)
+    need("a", iI128)
+    act(eI128m, A("I128m"), A("I128"), scale=0.125, bias=-0.9375)
+    act(eI128q, A("I128q"), A("I128"), scale=0.125, bias=-7.9375)
+    need("a", eZ)
+    inc(sc.dma_start(T.winM[:, 2048:2049], T.zero[:, 0:1]), eZd, 16)
 
     def rank_bias():
         e = ev()
-        inc(pe.matmul(T.b0[:, 0:64], T.pb[0:1, o1:o1 + 128], T.row[0:1, 0:64], True, False), e)
+        inc(pe.matmul(T.b0[:, 0:64], T.pb[0:2, o1:o1 + 128], T.row[0:2, 0:64], True, False), e)
         return e
 
     def rank_mm(E, e):
@@ -192,51 +203,40 @@ def rank_program(g, core, T, topo):
         for d in (1, 2, 3):
             inc(pe.matmul(T.b0[:, 16 * d:64], A("ones"), A(E, 0, 64 - 16 * d), False, d == 3), e)
 
-    need("p", eC1)
+    need("p", eOne, eRow)
     eRA = rank_bias()
 
-    need("v", eIx, eC1)
-    e1, eEA, e2, e3, e4, e5, s1, s2, s3, s4 = [ev() for _ in range(10)]
+    need("v", eIx, eRep)
+    e1, eEA, e2, e3, e4, s2, s3, s4 = [ev() for _ in range(8)]
     ts(e1, A("bI"), T.ix[:], 19, None, SR)
     need("v", e1)
-    tt(eEA, A("EA"), A("bI").indirect(T.rep[:, 0:4]), A("I16", 0, 64), OP.is_equal)
-    need("p", eEA)
+    tt(eEA, A("EA"), A("bI").indirect(T.rep[:, 0:4]), A("I16"), OP.is_equal)
+    need("p", eLp, eEA)
     rank_mm("EA", eRA)
+    ts(e2, A("iG"), T.ix[:], 14, None, AND)
     ts(e2, A("iPart"), T.ix[:], 18, 1, SR, AND)
     ts(e2, A("iCl"), T.ix[:], 4, MW - 1, SR, AND)
     ts(e2, A("iCh"), T.ix[:], 7, 2048 - MW, SR, AND)
-    ts(e2, A("iG"), T.ix[:], 14, None, AND)
-    need("v", eRA)
-    tt(s1, A("RA"), T.b0[:, 0:64], A("EA"), OP.mult)
+    need("v", iN2)
+    cp(eN2, T.N2h[:], A("N2f"))
+    need("v", eRst, eRA)
+    scan(s2, A("SA"), A("rst64"), T.b0[:, 0:64], OP.max)
     need("v", e2)
     ts(e3, A("dP"), A("iPart"), 2049.0, -2048.0, OP.mult, OP.add)
-    need("v", s1)
-    scan(s2, A("SA"), A("rst", 0, 64), A("RA"))
     tt(e3, A("dC"), A("iCl"), A("iCh"), OP.add)
     need("v", s2)
     rnd(s3, A("c16A"), A("SA", 15, 64, 16), 2)
+    tt(s4, A("mA"), A("SA", 15, 64, 16), A("iG"), OP.add)
     need("v", e3)
     tt(e4, A("delta"), A("dC"), A("dP"), OP.add)
-    need("v", s3)
-    tt(s4, A("hA"), A("SA", 15, 64, 16), A("c16A"), OP.subtract)
-    need("v", e4, iN2)
-    lb = [ev() for _ in range(4)]
-
-    def rhsA(k):
-        ts(lb[k], T.rA[:, 80 * k:80 * k + 80], A("N2"), A("c16A", k, k + 1), A("delta", k, k + 1), OP.is_equal, OP.mult)
-
-    rhsA(0)
-    need("v", s4)
-    tt(e5, A("mcol"), A("hA"), A("iG"), OP.add)
-    rhsA(1)
-    need("v", e5, eC2)
+    need("v", eN2, s3, e4, s4, eI128m)
     eSA = ev()
     for k in range(4):
-        if k > 1:
-            rhsA(k)
+        b = ev()
         l, r = T.lA[:, 128 * k:128 * k + 128], T.rA[:, 80 * k:80 * k + 80]
-        ts(lb[k], l, A("I128m"), A("mcol", k, k + 1), None, OP.is_equal)
-        need("p", lb[k])
+        ts(b, r, T.N2h[:], A("c16A", k, k + 1), A("delta", k, k + 1), OP.is_equal, OP.mult)
+        ts(b, l, A("I128m"), A("c16A", k, k + 1), A("mA", k, k + 1), OP.add, OP.is_equal)
+        need("p", b)
         inc(pe.matmul(T.b1[:, 0:80], l, r, k == 0, k == 3), eSA)
     need("v", eSA)
     eA1, eA2 = ev(), ev()
@@ -266,48 +266,51 @@ def rank_program(g, core, T, topo):
 
     iPI = iota(A("PI"), [[0, 2]], 0, 1)
     iI160 = iota(A("I160"), [[1, 160]], 0, 0)
-    iTC = iota(A("TC"), [[0, 4], [NT, 16]], 0, 0)
-    i32r = iota(A("I32r"), [[0, 4], [1, 32]], 0, 0)
+    iI16b = iota(A("I16b"), [[0, 10], [1, 16]], 0, 0)
+    iTC = iota(A("TC"), [[0, 4], [NT, 16]], int(BIG2), 0)
     iZ4 = iota(A("Z4"), [[1, 8], [0, 4]], 0, 0)
 
-    f1, f2, f3, f4, f5 = ev(), ev(), ev(), ev(), ev()
-    ts(f1, A("a0"), A("SA", 15, 64, 16), -7.0, None, OP.add)
+    f1, f2, f3, f4, f5, f6, f7 = [ev() for _ in range(7)]
+    k1, k2, kS, kI = ev(), ev(), ev(), ev()
+    ts(f1, A("a0"), A("SA", 15, 64, 16), -7.0 - BIG, None, OP.add)
     ts(f1, A("iNl"), T.ix[:], 1, None, AND)
     ts(f1, A("iNh"), T.ix[:], 13, 7, SR, AND)
-    ts(f1, A("I128q"), A("I128"), -63.5, 0.125, OP.add, OP.mult)
     need("v", f1)
     rnd(f2, A("u16"), A("a0"), 16)
     ts(f2, A("n1"), A("iNl"), 8.0, None, OP.mult)
+    need("v", iPI)
+    ts(k1, A("P15"), A("PI", 0, 1), 15, None, AND)
     need("v", f2)
     tt(f3, A("pl"), A("a0"), A("u16"), OP.subtract)
-    tt(f3, A("n2"), A("n1"), A("iNh"), OP.add)
-    need("v", f3)
-    tt(f4, A("qc"), A("n2"), A("u16"), OP.add)
-    need("v", f4, iI160, iPI)
-    for k in range(4):
-        ts(f5, T.lQ[:, 128 * k:128 * k + 128], A("I128q"), A("pl", k, k + 1), None, OP.is_equal)
-        ts(f5, T.rQ[:, 160 * k:160 * k + 160], A("I160"), A("qc", k, k + 1), None, OP.is_equal)
-    k1, k2, kS = ev(), ev(), ev()
-    ts(k1, A("P15"), A("PI", 0, 1), 15, None, AND)
-    ts(k1, A("P7"), A("PI", 0, 1), 7, None, AND)
-    ts(k1, A("PS3"), A("PI", 0, 1), 3, None, SR)
-    ts(k1, A("P3"), A("PI"), 3, None, AND)
-    ts(k1, A("ident"), A("JK"), 0.0, None, OP.is_equal)
-    ts(k1, A("U16"), A("I16", 0, 32), 16.0, None, OP.mult)
+    tt(f4, A("n2"), A("n1"), A("iNh"), OP.add)
     need("v", k1)
     cp(k2, A("PF", 0, 1), A("P15"))
-    cp(k2, A("PF", 1, 2), A("P7"))
-    cp(k2, A("PF", 2, 3), A("PS3"))
+    need("v", f4)
+    tt(f5, A("qc"), A("n2"), A("u16"), OP.add)
+    need("v", f3, eI128q)
+    for k in (0, 1):
+        ts(f6, T.lQ[:, 128 * k:128 * k + 128], A("I128q"), A("pl", k, k + 1), None, OP.is_equal)
     need("v", k2)
     ts(kS, A("S16"), A("I16", 0, 16), A("PF", 0, 1), None, OP.is_equal)
-    need("p", f5, k1)
+    ts(kI, A("ident"), A("JK"), 0.0, None, OP.is_equal)
+    need("v", f5, iI160)
+    for k in range(4):
+        ts(f6, T.rQ[:, 160 * k:160 * k + 160], A("I160"), A("qc", k, k + 1), None, OP.is_equal)
+    need("a", f3, eI128q)
+    fa = ev()
+    for k in (2, 3):
+        act(fa, A("abQ", 128 * (k - 2), 128 * (k - 1)), A("I128q"), FN.Abs, bias=A("pl", k, k + 1), scale=-1.0)
+    need("a", fa)
+    for k in (2, 3):
+        act(f7, T.lQ[:, 128 * k:128 * k + 128], A("abQ", 128 * (k - 2), 128 * (k - 1)), FN.Relu, bias=1.0, scale=-8.0)
+    need("p", f6, f7, kI)
     eQ, eTr, eTk = ev(), ev(), ev()
     for k in range(4):
         inc(pe.matmul(T.b2[:, 0:160], T.lQ[:, 128 * k:128 * k + 128], T.rQ[:, 160 * k:160 * k + 160], k == 0, k == 3), eQ)
     for k in range(4):
         inc(pe.transpose(T.b6[:, 128 * k:128 * k + 128], T.lQ[:, 128 * k:128 * k + 128], A("ident")), eTr)
     need("a", eTr)
-    acp(eTk, T.Tk[:], T.b6[:, 0:512])
+    act(eTk, T.Tk[:], T.b6[:, 0:512])
 
     eMa = ev(T.sem.mArr, 2 * nfull + nstay)
     need("v", eMa, aArr, eA1, eA2, eZd, *eM)
@@ -316,20 +319,23 @@ def rank_program(g, core, T, topo):
     for p, (members, bank) in enumerate(((phases[0], T.b3), (phases[1], T.b4), ([me], T.b7))):
         e = ev()
         for n, i in enumerate(members):
-            b = ev()
-            cp(b, T.G[:, SZ * i:SZ * i + SZ], T.winM[:, 0:NM].indirect(T.offA[:, W * i:W * i + W]))
-            need("p", b)
-            for u in (0, 1):
-                inc(pe.matmul(bank[:, 32 * n + 16 * u:32 * n + 16 * u + 16], T.G[:, SZ * i + 128 * u:SZ * i + 128 * u + 128], A("S16"), True, True), e)
+            cuts = 2 if p == 1 and n == 1 else 1
+            for h in range(cuts):
+                b = ev()
+                a, w = 256 // cuts * h, 256 // cuts
+                cp(b, T.G[:, SZ * i + a:SZ * i + a + w], T.winM[:, 0:NM].indirect(T.offA[:, W * i + a // 16:W * i + (a + w) // 16]))
+                need("p", b)
+                for u in range(a // 128, (a + w) // 128):
+                    inc(pe.matmul(bank[:, 32 * n + 16 * u:32 * n + 16 * u + 16], T.G[:, SZ * i + 128 * u:SZ * i + 128 * u + 128], A("S16"), True, True), e)
         if members == [me]:
             need("v", e)
             cp(eB2, T.landB[:, 32 * me:32 * me + 32], bank[:, 0:32])
         else:
             need("a", e)
             c = ev()
-            acp(c, T.sendB[:, 64 * p:64 * p + 64], bank[:, 0:64])
+            act(c, T.sendB[:, 64 * p:64 * p + 64], bank[:, 0:64])
             need("g", c)
-            locB.append(send(members, T.sendB, [2 * p, 2 * p + 1], T.landB, 32, T.sem.bArr))
+            locB.append(send(members, T.sendB, [2 * p, 2 * p + 1], T.landB, 32, [T.sem.bArr0, T.sem.bArr1][p]))
 
     need("y", *locB)
     load_table(3)
@@ -338,74 +344,100 @@ def rank_program(g, core, T, topo):
         need("g", eT[q])
         exchange(T.winT, t0 + 2048 * q, t0 + 2048 * q + 2048, T.sem.tArr, eTx, full)
 
-    need("v", iTC, i32r, iZ4)
-    k3, k3r = ev(), ev()
+    k3, k3r, k4, kA, kR = ev(), ev(), ev(), ev(), ev()
+    need("a", iI16b)
+    act(kR, A("rst"), A("I16b"), FN.Sign)
+    act(kR, A("HL"), A("I16b", 0, 32), scale=0.0)
+    act(kA, A("I16m"), A("I16b", 0, 128), scale=0.125, bias=-0.9375)
+    fill(k3r, T.row[0:2, 128:192], 4.0)
+    ts(k4, A("P7"), A("PI", 0, 1), 7, None, AND)
+    ts(k4, A("PS3"), A("PI", 0, 1), 3, None, SR)
+    ts(k4, A("P3"), A("PI"), 3, None, AND)
+    need("v", eU16)
     for k in range(4):
-        ts(k3, A("mask2", 32 * k, 32 * k + 32), A("U16"), A("u16", k, k + 1), None, OP.is_equal)
-    inc(v.memset(A("HL"), 0.0), k3)
-    inc(v.memset(T.row[0:1, 128:256], -NT * 4.0), k3r)
+        ts(k3, A("mask2", 16 * k, 16 * k + 16), A("U16"), A("u16", k, k + 1), BIG2, OP.is_equal, OP.mult)
     need("v", k3r)
-    for k in range(4):
-        inc(v.memset(T.row[0:1, 144 + 32 * k:160 + 32 * k], 4.0), k3)
-    ts(k3, A("rst32"), A("I32r"), 0.0, None, OP.is_gt)
-    ts(k3, A("I16m"), A("I16", 0, 128), -7.5, 0.125, OP.add, OP.mult)
-    cp(k3, T.repF[:], A("P3"))
-    ts(k3, T.lF[:], A("I16", 0, 128), A("PF", 2, 3), None, OP.is_equal)
-    ts(k3, A("Z0"), A("Z4"), A("PF", 1, 2), None, OP.is_equal)
-    need("v", k3)
+    fill(k3, T.row[0:1, 128:192], -NT * 4.0)
+    need("v", k4, k3, iTC, iI16b, iZ4)
     need("p", k3)
     eDm = ev()
-    inc(pe.matmul(T.b5[:, 0:128], T.pb[0:1, o1:o1 + 128], T.row[0:1, 128:256], True, False), eDm)
+    inc(pe.matmul(T.b5[:, 0:64], T.pb[0:2, o1:o1 + 128], T.row[0:2, 128:192], True, False), eDm)
+    inc(pe.matmul(T.b5[:, 0:64], A("ident"), A("mask2"), False, False), eDm)
     eRC = rank_bias()
+    k5, k6 = ev(), ev()
+    cp(k5, A("PF", 1, 2), A("P7"))
+    cp(k5, A("PF", 2, 3), A("PS3"))
+    cp(k6, T.repF[:], A("P3"))
+    need("v", k5)
+    ts(k6, T.lF[:], A("I16b", 0, 128), A("PF", 2, 3), None, OP.is_equal)
+    ts(k6, A("Z0"), A("Z4"), A("PF", 1, 2), None, OP.is_equal)
 
-    need("v", bArr, eB2, eQ)
-    x1, x2, x3, x4, x5, x6, x7, x8, x9, x10, x11, x12 = [ev() for _ in range(12)]
-    tt(x1, A("X"), T.landB[:], T.b2[:, 0:160], OP.mult)
-    need("v", x1)
-    scan(x2, A("SX"), A("rst"), A("X"))
-    need("v", x2)
+    x3, x4, x6, x7, x8, x9, x10, x12, y5, y7 = [ev() for _ in range(10)]
+    need("v", eB2, eQ, kR)
+    for p in (0, 1):
+        blocks = [i for i in range(nl) if (i in early) == (p == 0)]
+        runs = []
+        for i in blocks:
+            if runs and runs[-1][1] == i:
+                runs[-1][1] = i + 1
+            else:
+                runs.append([i, i + 1])
+        need("v", bArr[p])
+        x1, x2 = ev(), ev()
+        for a, b in runs:
+            tt(x1, A("X", 32 * a, 32 * b), T.landB[:, 32 * a:32 * b], T.b2[:, 32 * a:32 * b], OP.mult)
+        need("v", x1)
+        for a, b in runs:
+            scan(x2, A("SX", 32 * a, 32 * b), A("rst", 32 * a, 32 * b), A("X", 32 * a, 32 * b), OP.add)
+        need("v", x2)
     rnd(x3, A("HL", 0, 10), A("SX", 15, 160, 16), 512)
     need("v", x3)
     tt(x4, A("HL", 16, 26), A("SX", 15, 160, 16), A("HL", 0, 10), OP.subtract)
-    need("p", x3, x4, eTk)
-    for k in range(4):
-        inc(pe.matmul(T.b5[:, 32 * k:32 * k + 32], T.Tk[:, 128 * k:128 * k + 128], A("HL"), False, k == 3), eDm)
+    for w, e in ((0, x3), (1, x4)):
+        need("p", e, eTk)
+        for k in range(4):
+            inc(pe.matmul(T.b5[:, 16 * k:16 * k + 16], T.Tk[:, 128 * k:128 * k + 128], A("HL", 16 * w, 16 * w + 16), False, w == 1 and k == 3), eDm)
     need("v", eDm)
-    tt(x5, A("D1"), T.b5[:, 0:128], A("mask2"), OP.mult)
-    need("v", x5)
-    scan(x6, A("SD"), A("rst32"), A("D1"))
+    scan(x6, A("SD"), A("rst64"), T.b5[:, 0:64], OP.max)
     need("v", x6)
-    rnd(x7, A("tU"), A("SD", 31, 128, 32), NT)
+    rnd(x7, A("tU"), A("SD", 15, 64, 16), NT)
     need("v", x7)
     eEC = ev()
     tt(eEC, A("EC"), A("tU").indirect(T.rep[:, 0:4]), A("TC"), OP.is_equal)
     need("p", eEC)
     rank_mm("EC", eRC)
-    tt(x8, A("lc"), A("SD", 31, 128, 32), A("tU"), OP.subtract)
+    tt(x8, A("lc"), A("SD", 15, 64, 16), A("tU"), OP.subtract)
     need("v", x8)
-    rnd(x9, A("hi2"), A("lc"), 64)
+    rnd(x9, A("hi2"), A("lc"), 64, -64.0)
     need("v", eRC)
-    tt(x11, A("RC"), T.b0[:, 0:64], A("EC"), OP.mult)
+    scan(x12, A("SC"), A("rst64"), T.b0[:, 0:64], OP.max)
     need("v", x9)
     tt(x10, A("lo2"), A("lc"), A("hi2"), OP.subtract)
-    need("v", x11)
-    scan(x12, A("SC"), A("rst", 0, 64), A("RC"))
     need("v", x12)
-    y1, y2, y3, y4, y5, y6 = ev(), ev(), ev(), ev(), ev(), ev()
     rnd(y5, A("c16C"), A("SC", 15, 64, 16), 2)
-    need("v", y5)
-    tt(y6, A("sC"), A("SC", 15, 64, 16), A("c16C"), OP.subtract)
     need("v", x10)
+    ts(y7, A("lon"), A("lo2"), -1.0, None, OP.mult)
+    need("v", y5, kA)
+    sa, sb = ev(), [ev(), ev()]
+    need("a", y5)
+    for k in (2, 3):
+        act(sa, A("abC", 80 * (k - 2), 80 * (k - 1)), A("N2f"), FN.Abs, bias=A("c16C", k, k + 1), scale=-1.0)
+    need("a", sa, x10, y7)
+    for k in (2, 3):
+        act(sb[k - 2], T.rC[:, 160 * k + 80:160 * k + 160], A("abC", 80 * (k - 2), 80 * (k - 1)), FN.Relu,
+            bias=A("lo2", k, k + 1), scale=A("lon", k, k + 1))
     eSC = ev()
     for k in range(4):
         b = ev()
         l, r = T.lC[:, 128 * k:128 * k + 128], [T.rC[:, 160 * k + 80 * q:160 * k + 80 * q + 80] for q in (0, 1)]
-        ts(b, r[0], A("N2"), A("c16C", k, k + 1), A("hi2", k, k + 1), OP.is_equal, OP.mult)
-        ts(b, r[1], A("N2"), A("c16C", k, k + 1), A("lo2", k, k + 1), OP.is_equal, OP.mult)
-        need("v", y6)
-        ts(b, l, A("I16m"), A("sC", k, k + 1), None, OP.is_equal)
+        ts(b, r[0], T.N2h[:], A("c16C", k, k + 1), A("hi2", k, k + 1), OP.is_equal, OP.mult)
+        if k < 2:
+            ts(b, r[1], T.N2h[:], A("c16C", k, k + 1), A("lo2", k, k + 1), OP.is_equal, OP.mult)
+        ts(b, l, A("I16m"), A("c16C", k, k + 1), A("SC", 16 * k + 15, 16 * k + 16), OP.add, OP.is_equal)
         need("p", b)
         for q in (0, 1):
+            if k > 1 and q == 1:
+                need("p", sb[k - 2])
             inc(pe.matmul(T.b1[:, 0:80], l, r[q], k == 0 and q == 0, k == 3 and q == 1), eSC)
     need("v", eSC)
     eCs1, eCs2 = ev(), ev()
@@ -414,8 +446,9 @@ def rank_program(g, core, T, topo):
     need("g", eCs1)
     locC = send(order, T.sendC, order, T.offC, W, T.sem.cArr)
 
-    ts(y1, A("slotC"), A("SC", 15, 64, 16), 8.0, 7.5, OP.mult, OP.add)
-    need("v", y1)
+    y1, y2, y3, y4 = ev(), ev(), ev(), ev()
+    ts(y1, A("slotC"), A("SC", 15, 64, 16), 8.0, 7.5 - 8.0 * BIG, OP.mult, OP.add)
+    need("v", y1, k6)
     tt(y2, T.rF[:], A("slotC").indirect(T.repF[:, 0:2]), A("Z0"), OP.mult)
     need("p", y2)
     inc(pe.matmul(T.b7[:, 0:32], T.lF[:], T.rF[:], True, True), y3)
@@ -425,23 +458,31 @@ def rank_program(g, core, T, topo):
     eTa = ev(T.sem.tArr, 4 * nfull)
     for q in ("v", "a"):
         need(q, eTa, cArr, eCs2, *eT)
-    for members in phases:
+
+    def serve(i, dst, e):
+        for n in (0, 1):
+            a = SZ * i + 128 * n
+            src = T.winT[:, 0:NT].indirect(T.offC[:, W * i + 8 * n:W * i + 8 * n + 8])
+            (cp, act)[n](e[n], dst[:, a:a + 128], src)
+
+    for members in (order[0:1], order[1:2], order[2:4]):
         e = [ev(), ev()]
-        for n, i in enumerate(members):
-            src = T.winT[:, 0:NT].indirect(T.offC[:, W * i:W * i + W])
-            (cp, acp)[n](e[n], T.sendD[:, SZ * i:SZ * i + SZ], src)
+        if len(members) == 1:
+            serve(members[0], T.sendD, e)
+        else:
+            for n, i in enumerate(members):
+                src = T.winT[:, 0:NT].indirect(T.offC[:, W * i:W * i + W])
+                (cp, act)[n](e[n], T.sendD[:, SZ * i:SZ * i + SZ], src)
         need("g", *e)
         send(members, T.sendD, members, T.landD, SZ, T.sem.dArr)
     eD = [ev(), ev()]
-    for n in (0, 1):
-        a = SZ * me + 128 * n
-        (cp, acp)[n](eD[n], T.landD[:, a:a + 128], T.winT[:, 0:NT].indirect(T.offC[:, W * me + 8 * n:W * me + 8 * n + 8]))
+    serve(me, T.landD, eD)
 
     for q in ("v", "a"):
         need(q, dArr, y4, *eD)
     eY1, eY2, eS1, eS2 = ev(), ev(), ev(), ev()
     cp(eY1, T.yo[:, 0:256], T.landD[:, 0:1280].indirect(T.offF[:, 0:16]))
-    acp(eY2, T.yo[:, 256:512], T.landD[:, 0:1280].indirect(T.offF[:, 16:32]))
+    act(eY2, T.yo[:, 256:512], T.landD[:, 0:1280].indirect(T.offF[:, 16:32]))
     need("y", eY1)
     inc(sy.dma_start(T.y[:, 0:256], T.yo[:, 0:256]), eS1, 16)
     need("a", eY2)

@@ -30,12 +30,12 @@ SCRATCH = {
 PACK = {
     ("pf", F32): [("dP", 4), ("dC", 4), ("delta", 4), ("c16A", 4), ("mA", 4), ("a0", 4), ("u16", 4),
                   ("pl", 4), ("n1", 4), ("n2", 4), ("qc", 4), ("tU", 4), ("lc", 4), ("hi2", 4), ("lo2", 4), ("lon", 4),
-                  ("c16C", 4), ("slotC", 4), ("PF", 4), ("S16", 16), ("Z0", 32), ("SA", 64), ("SC", 64),
-                  ("X", 160), ("SX", 160), ("SD", 64), ("N2f", 80)],
+                  ("c16C", 4), ("slotC", 4), ("PF", 4), ("S16", 16), ("S16a", 16), ("S16b", 16), ("Z0", 32),
+                  ("SA", 64), ("SC", 64), ("keep", 160), ("SX", 160), ("SD", 64), ("N2f", 80)],
     ("pi", I32): [("bI", 4), ("iPart", 4), ("iCl", 4), ("iCh", 4), ("iG", 4), ("iNl", 4), ("iNh", 4), ("PI", 2),
                   ("P3", 2), ("P15", 1), ("P7", 1), ("PS3", 1)],
     ("pb", BF): [("I16", 64), ("I16b", 160), ("I128", 128), ("JK", 128), ("I160", 160), ("TC", 64), ("Z4", 32),
-                 ("ones", 128), ("Lt", 128), ("Lu", 128), ("Lp", 128), ("ident", 128), ("rst64", 64), ("rst", 160),
+                 ("ones", 128), ("Lt", 128), ("Lu", 128), ("Lp", 128), ("ident", 128), ("rst64", 64),
                  ("I16m", 128), ("I128m", 128), ("I128q", 128), ("U16", 16), ("EA", 64), ("EC", 64), ("HL", 32),
                  ("mask2", 64), ("abQ", 256), ("abC", 160)],
 }
@@ -49,7 +49,7 @@ for (_b, _d), _l in PACK.items():
 for _k in (0, 1, 2, 3, 4, 5, 7):
     SCRATCH["b%d" % _k] = ("psum", [128, 512], F32)
 SCRATCH["b6"] = ("psum", [128, 1024], BF)
-SEMAPHORES = ["mArr", "aArr", "bArr0", "bArr1", "tArr", "cArr", "dArr"] + ["e%d" % i for i in range(NEV)]
+SEMAPHORES = ["mArr", "aArr", "bArr0", "bArr1", "tArr", "cArr0", "cArr1", "dArr"] + ["e%d" % i for i in range(NEV)]
 
 OP = AluOpType
 SR, AND = OP.logical_shift_right, OP.bitwise_and
@@ -73,18 +73,20 @@ def rank_program(g, core, T, topo):
     lane = [[c for c in cores if topo.chip(c) == ch and topo.die(c) == topo.die(core)][0] for ch in chips]
     nl, me = len(lane), lane.index(core)
     order = [(me + d) % nl for d in range(1, nl)]
-    phases = [order[0:2], order[2:4]]
-    early = [me] + [(me - d) % nl for d in (1, 2)]
+    early = [(me - d) % nl for d in (1, 2)]
 
     def A(name, a=0, b=None, step=1):
         buf, o, w = PLACE[name]
         b = w if b is None else b
         return T[buf][:, o + a:o + b:step] if step > 1 else T[buf][:, o + a:o + b]
 
-    groups, waited = [], {}
+    groups, waited, own = [], {}, []
 
     def ev(sem=None, n=0):
-        e = {"s": sem if sem is not None else T.sem["e%d" % len(groups)], "n": n, "k": len(groups)}
+        if sem is None:
+            sem = T.sem["e%d" % len(own)]
+            own.append(sem)
+        e = {"s": sem, "n": n, "k": len(groups)}
         groups.append(e)
         return e
 
@@ -140,12 +142,12 @@ def rank_program(g, core, T, topo):
 
     leave = topo.mask(core, lane[order[0]])
     noff = len(bits(leave))
-    aArr, cArr = ev(T.sem.aArr, noff), ev(T.sem.cArr, noff)
-    bArr = [ev(T.sem.bArr0, noff), ev(T.sem.bArr1, noff)]
+    aArr = ev(T.sem.aArr, noff)
+    bArr = [ev(T.sem.bArr0, noff), ev(T.sem.bArr1, 2 * noff)]
+    cArr = [ev(T.sem.cArr0, noff), ev(T.sem.cArr1, noff)]
     dArr = ev(T.sem.dArr, 3 * noff)
     full = topo.mask(core, partner)
     stay = full & ~leave
-    nfull, nstay = len(bits(full)), len(bits(stay))
     prid, ppid, _ = topo.addr(partner)
 
     def exchange(buf, a, b, rsem, e, mask):
@@ -159,6 +161,11 @@ def rank_program(g, core, T, topo):
     for h in range(MC):
         eM.append(ev())
         inc(sy.dma_start(T.winM[:, m0 + h * MW:m0 + (h + 1) * MW], T.mp[:, h * 8 * MW:(h + 1) * 8 * MW]), eM[h], 16)
+    t0 = 8192 * part
+    eT = [ev(), ev(), ev(), ev()]
+
+    def load_table(q):
+        inc(sy.dma_start(T.winT[:, t0 + 2048 * q:t0 + 2048 * q + 2048], T.tab[:, 2048 * q:2048 * q + 2048]), eT[q], 16)
 
     def iota(out, pattern, base, cm):
         e = ev()
@@ -168,6 +175,7 @@ def rank_program(g, core, T, topo):
     iJK = iota(A("JK"), [[1, 128]], 0, -1)
     iN2 = iota(A("N2f"), [[2, 80]], int(BIG), 0)
     iI128 = iota(A("I128"), [[1, 128]], 0, 0)
+    iPI = iota(A("PI"), [[0, 2]], 0, 1)
 
     o1, o16 = PLACE["ones"][1], PLACE["I16"][1]
     eOne, eRep, eR0, eRow, eZ, eZd, eL, eLp, eN2 = [ev() for _ in range(9)]
@@ -244,19 +252,14 @@ def rank_program(g, core, T, topo):
     ts(eA2, T.offA[:, W * me:W * me + W], T.b1[:, W * me:W * me + W], 2048.0, None, OP.add)
 
     eMx = ev()
-    for h, mask in ((0, full), (1, stay)):
+    for h, mask in ((0, full), (1, full), (2, stay)):
         need("g", eM[h])
         exchange(T.winM, m0 + h * MW, m0 + (h + 1) * MW, T.sem.mArr, eMx, mask)
     need("g", eA1)
     locA = send(order, T.sendA, order, T.offA, W, T.sem.aArr)
     need("g", *eM)
-    exchange(T.winM, m0 + 2 * MW, m0 + 2048, T.sem.mArr, eMx, full)
-
-    t0 = 8192 * part
-    eT = [ev(), ev(), ev(), ev()]
-
-    def load_table(q):
-        inc(sy.dma_start(T.winT[:, t0 + 2048 * q:t0 + 2048 * q + 2048], T.tab[:, 2048 * q:2048 * q + 2048]), eT[q], 16)
+    exchange(T.winM, m0 + 3 * MW, m0 + 2048, T.sem.mArr, eMx, full)
+    mapsent = ev(T.sem.mArr, eMx["n"])
 
     need("y", locA)
     load_table(0)
@@ -264,34 +267,36 @@ def rank_program(g, core, T, topo):
     need("y", eT[0], eT[1])
     load_table(2)
 
-    iPI = iota(A("PI"), [[0, 2]], 0, 1)
     iI160 = iota(A("I160"), [[1, 160]], 0, 0)
     iI16b = iota(A("I16b"), [[0, 10], [1, 16]], 0, 0)
     iTC = iota(A("TC"), [[0, 4], [NT, 16]], int(BIG2), 0)
     iZ4 = iota(A("Z4"), [[1, 8], [0, 4]], 0, 0)
 
     f1, f2, f3, f4, f5, f6, f7 = [ev() for _ in range(7)]
-    k1, k2, kS, kI = ev(), ev(), ev(), ev()
+    k1, k2, kS, kT, kI = ev(), ev(), ev(), ev(), ev()
     ts(f1, A("a0"), A("SA", 15, 64, 16), -7.0 - BIG, None, OP.add)
     ts(f1, A("iNl"), T.ix[:], 1, None, AND)
     ts(f1, A("iNh"), T.ix[:], 13, 7, SR, AND)
+    need("v", iPI, iI128)
+    ts(k1, A("P15"), A("PI", 0, 1), 15, None, AND)
     need("v", f1)
     rnd(f2, A("u16"), A("a0"), 16)
     ts(f2, A("n1"), A("iNl"), 8.0, None, OP.mult)
-    need("v", iPI)
-    ts(k1, A("P15"), A("PI", 0, 1), 15, None, AND)
+    need("v", k1)
+    cp(k2, A("PF", 0, 1), A("P15"))
     need("v", f2)
     tt(f3, A("pl"), A("a0"), A("u16"), OP.subtract)
     tt(f4, A("n2"), A("n1"), A("iNh"), OP.add)
-    need("v", k1)
-    cp(k2, A("PF", 0, 1), A("P15"))
+    need("v", k2)
+    ts(kT, A("S16a"), A("I16", 0, 16), A("PF", 0, 1), None, OP.is_equal)
+    ts(kT, A("S16b"), A("I128", 1, 17), A("PF", 0, 1), None, OP.is_equal)
     need("v", f4)
     tt(f5, A("qc"), A("n2"), A("u16"), OP.add)
+    need("v", kT)
+    tt(kS, A("S16"), A("S16a"), A("S16b"), OP.subtract)
     need("v", f3, eI128q)
     for k in (0, 1):
         ts(f6, T.lQ[:, 128 * k:128 * k + 128], A("I128q"), A("pl", k, k + 1), None, OP.is_equal)
-    need("v", k2)
-    ts(kS, A("S16"), A("I16", 0, 16), A("PF", 0, 1), None, OP.is_equal)
     ts(kI, A("ident"), A("JK"), 0.0, None, OP.is_equal)
     need("v", f5, iI160)
     for k in range(4):
@@ -304,38 +309,50 @@ def rank_program(g, core, T, topo):
     for k in (2, 3):
         act(f7, T.lQ[:, 128 * k:128 * k + 128], A("abQ", 128 * (k - 2), 128 * (k - 1)), FN.Relu, bias=1.0, scale=-8.0)
     need("p", f6, f7, kI)
-    eQ, eTr, eTk = ev(), ev(), ev()
+    eQ, eTr, eTk, eKeep = ev(), ev(), ev(), ev()
     for k in range(4):
         inc(pe.matmul(T.b2[:, 0:160], T.lQ[:, 128 * k:128 * k + 128], T.rQ[:, 160 * k:160 * k + 160], k == 0, k == 3), eQ)
     for k in range(4):
         inc(pe.transpose(T.b6[:, 128 * k:128 * k + 128], T.lQ[:, 128 * k:128 * k + 128], A("ident")), eTr)
-    need("a", eTr)
-    act(eTk, T.Tk[:], T.b6[:, 0:512])
 
-    eMa = ev(T.sem.mArr, 2 * nfull + nstay)
-    need("v", eMa, aArr, eA1, eA2, eZd, *eM)
+    for q in ("v", "a"):
+        need(q, mapsent, aArr, eA1, eA2, eZd, *eM)
     need("p", kS)
     locB, eB2 = [], ev()
-    for p, (members, bank) in enumerate(((phases[0], T.b3), (phases[1], T.b4), ([me], T.b7))):
+
+    def fetch(members, bank, before=()):
         e = ev()
         for n, i in enumerate(members):
-            cuts = 2 if p == 1 and n == 1 else 1
-            for h in range(cuts):
+            for u in (0, 1):
                 b = ev()
-                a, w = 256 // cuts * h, 256 // cuts
-                cp(b, T.G[:, SZ * i + a:SZ * i + a + w], T.winM[:, 0:NM].indirect(T.offA[:, W * i + a // 16:W * i + (a + w) // 16]))
-                need("p", b)
-                for u in range(a // 128, (a + w) // 128):
-                    inc(pe.matmul(bank[:, 32 * n + 16 * u:32 * n + 16 * u + 16], T.G[:, SZ * i + 128 * u:SZ * i + 128 * u + 128], A("S16"), True, True), e)
-        if members == [me]:
-            need("v", e)
-            cp(eB2, T.landB[:, 32 * me:32 * me + 32], bank[:, 0:32])
-        else:
-            need("a", e)
-            c = ev()
-            act(c, T.sendB[:, 64 * p:64 * p + 64], bank[:, 0:64])
-            need("g", c)
-            locB.append(send(members, T.sendB, [2 * p, 2 * p + 1], T.landB, 32, [T.sem.bArr0, T.sem.bArr1][p]))
+                a, o = SZ * i + 128 * u, W * i + 8 * u
+                (cp, act)[u](b, T.G[:, a:a + 128], T.winM[:, 0:NM].indirect(T.offA[:, o:o + 8]))
+                need("p", b, *before)
+                inc(pe.matmul(bank[:, 32 * n + 16 * u:32 * n + 16 * u + 16], T.G[:, a:a + 128], A("S16"), True, True), e)
+        return e
+
+    def answer(q, e, members, bank, o, rsem):
+        c, n = ev(), len(members)
+        need(q, e)
+        (cp if q == "v" else act)(c, T.sendB[:, 32 * o:32 * (o + n)], bank[:, 0:32 * n])
+        need("g", c)
+        locB.append(send(members, T.sendB, [o + k for k in range(n)], T.landB, 32, rsem))
+        return c
+
+    m = [order[0:2], order[2:3], order[3:4]]
+    b0 = fetch(m[0], T.b3)
+    b1 = fetch(m[1], T.b4)
+    c0 = answer("v", b0, m[0], T.b3, 0, T.sem.bArr0)
+    b2 = fetch(m[2], T.b7)
+    answer("a", b1, m[1], T.b4, 2, T.sem.bArr1)
+    answer("a", b2, m[2], T.b7, 3, T.sem.bArr1)
+    b3 = fetch([me], T.b3, [c0])
+    need("v", b3)
+    cp(eB2, T.landB[:, 32 * me:32 * me + 32], T.b3[:, 0:32])
+    need("a", eQ)
+    act(eKeep, A("keep"), T.b2[:, 0:160], scale=-1.0, bias=1.0)
+    need("a", eTr)
+    act(eTk, T.Tk[:], T.b6[:, 0:512])
 
     need("y", *locB)
     load_table(3)
@@ -346,7 +363,6 @@ def rank_program(g, core, T, topo):
 
     k3, k3r, k4, kA, kR = ev(), ev(), ev(), ev(), ev()
     need("a", iI16b)
-    act(kR, A("rst"), A("I16b"), FN.Sign)
     act(kR, A("HL"), A("I16b", 0, 32), scale=0.0)
     act(kA, A("I16m"), A("I16b", 0, 128), scale=0.125, bias=-0.9375)
     fill(k3r, T.row[0:2, 128:192], 4.0)
@@ -372,8 +388,8 @@ def rank_program(g, core, T, topo):
     ts(k6, T.lF[:], A("I16b", 0, 128), A("PF", 2, 3), None, OP.is_equal)
     ts(k6, A("Z0"), A("Z4"), A("PF", 1, 2), None, OP.is_equal)
 
-    x3, x4, x6, x7, x8, x9, x10, x12, y5, y7 = [ev() for _ in range(10)]
-    need("v", eB2, eQ, kR)
+    x2, x3, x4, x6, x7, x8, x9, x10, x12, y5, y7 = [ev() for _ in range(11)]
+    need("v", eB2, eKeep, kR)
     for p in (0, 1):
         blocks = [i for i in range(nl) if (i in early) == (p == 0)]
         runs = []
@@ -383,13 +399,9 @@ def rank_program(g, core, T, topo):
             else:
                 runs.append([i, i + 1])
         need("v", bArr[p])
-        x1, x2 = ev(), ev()
         for a, b in runs:
-            tt(x1, A("X", 32 * a, 32 * b), T.landB[:, 32 * a:32 * b], T.b2[:, 32 * a:32 * b], OP.mult)
-        need("v", x1)
-        for a, b in runs:
-            scan(x2, A("SX", 32 * a, 32 * b), A("rst", 32 * a, 32 * b), A("X", 32 * a, 32 * b), OP.add)
-        need("v", x2)
+            scan(x2, A("SX", 32 * a, 32 * b), A("keep", 32 * a, 32 * b), T.landB[:, 32 * a:32 * b], OP.add)
+    need("v", x2)
     rnd(x3, A("HL", 0, 10), A("SX", 15, 160, 16), 512)
     need("v", x3)
     tt(x4, A("HL", 16, 26), A("SX", 15, 160, 16), A("HL", 0, 10), OP.subtract)
@@ -444,20 +456,21 @@ def rank_program(g, core, T, topo):
     ts(eCs1, T.sendC[:], T.b1[:, 0:80], NT / 2 - 0.5, None, OP.add)
     ts(eCs2, T.offC[:, W * me:W * me + W], T.b1[:, W * me:W * me + W], NT / 2 - 0.5, None, OP.add)
     need("g", eCs1)
-    locC = send(order, T.sendC, order, T.offC, W, T.sem.cArr)
+    send(order[2:4], T.sendC, order[2:4], T.offC, W, T.sem.cArr0)
+    send(order[0:2], T.sendC, order[0:2], T.offC, W, T.sem.cArr1)
 
     y1, y2, y3, y4 = ev(), ev(), ev(), ev()
     ts(y1, A("slotC"), A("SC", 15, 64, 16), 8.0, 7.5 - 8.0 * BIG, OP.mult, OP.add)
     need("v", y1, k6)
     tt(y2, T.rF[:], A("slotC").indirect(T.repF[:, 0:2]), A("Z0"), OP.mult)
     need("p", y2)
-    inc(pe.matmul(T.b7[:, 0:32], T.lF[:], T.rF[:], True, True), y3)
+    inc(pe.matmul(T.b3[:, 0:32], T.lF[:], T.rF[:], True, True), y3)
     need("v", y3)
-    cp(y4, T.offF[:], T.b7[:, 0:32])
+    cp(y4, T.offF[:], T.b3[:, 0:32])
 
-    eTa = ev(T.sem.tArr, 4 * nfull)
+    eTa = ev(T.sem.tArr, eTx["n"])
     for q in ("v", "a"):
-        need(q, eTa, cArr, eCs2, *eT)
+        need(q, eTa, eCs2, *eT)
 
     def serve(i, dst, e):
         for n in (0, 1):
@@ -465,7 +478,9 @@ def rank_program(g, core, T, topo):
             src = T.winT[:, 0:NT].indirect(T.offC[:, W * i + 8 * n:W * i + 8 * n + 8])
             (cp, act)[n](e[n], dst[:, a:a + 128], src)
 
-    for members in (order[0:1], order[1:2], order[2:4]):
+    for p, members in enumerate((order[0:1], order[1:2], order[2:4])):
+        for q in ("v", "a"):
+            need(q, cArr[p // 2])
         e = [ev(), ev()]
         if len(members) == 1:
             serve(members[0], T.sendD, e)

import numpy as np
from concourse.bass import DstId, RemoteDMATransfer
from concourse.mybir import dt, AluOpType, ActivationFunctionType

MC = 4
MW = 2048 // MC
NM = 4097
NT = 16384
SZ, W = 256, 16
NEV = 142
BIG = 512.0
BIG2 = 262144.0
F32, BF, FP, I32, U16 = "float32", "bfloat16", "float16", "int32", "uint16"


def _sb(n, d):
    return ("sbuf", [128, n], d)


SCRATCH = {
    "winM": _sb(NM + 3, I32), "winT": _sb(NT, BF), "zero": _sb(4, I32), "ix": _sb(4, I32),
    "row": _sb(256, BF),
    "lA": _sb(512, FP), "rA": _sb(320, FP), "N2h": _sb(80, FP), "lF": _sb(128, FP), "rF": _sb(32, FP),
    "lQ": _sb(512, BF), "rQ": _sb(640, BF), "Tk": _sb(512, BF), "lC": _sb(512, BF), "rC": _sb(640, BF),
    "rep": _sb(4, U16), "repF": _sb(2, U16), "offF": _sb(32, U16),
    "sendA": _sb(80, U16), "offA": _sb(80, U16), "sendC": _sb(80, U16), "offC": _sb(80, U16),
    "G": _sb(1280, F32), "sendB": _sb(128, F32), "landB": _sb(160, F32),
    "sendD": _sb(1280, BF), "landD": _sb(1280, BF), "yo": _sb(512, BF),
}
PACK = {
    ("pf", F32): [("dP", 4), ("dC", 4), ("delta", 4), ("c16A", 4), ("mA", 4), ("a0", 4), ("u16", 4),
                  ("pl", 4), ("n1", 4), ("n2", 4), ("qc", 4), ("tU", 4), ("lc", 4), ("hi2", 4), ("lo2", 4), ("lon", 4),
                  ("c16C", 4), ("slotC", 4), ("PF", 4), ("S16", 16), ("S16a", 16), ("S16b", 16), ("Z0", 32),
                  ("SA", 64), ("SC", 64), ("keep", 160), ("SX", 160), ("SD", 64), ("N2f", 80)],
    ("pi", I32): [("bI", 4), ("iPart", 4), ("iCl", 4), ("iCh", 4), ("iG", 4), ("iNl", 4), ("iNh", 4), ("PI", 2),
                  ("P3", 2), ("P15", 1), ("P7", 1), ("PS3", 1)],
    ("pb", BF): [("I16", 64), ("I16b", 160), ("I128", 128), ("JK", 128), ("I160", 160), ("TC", 64), ("Z4", 32),
                 ("ones", 128), ("Lt", 128), ("Lu", 128), ("Lp", 128), ("ident", 128), ("rst64", 64),
                 ("I16m", 128), ("I128m", 128), ("I128q", 128), ("U16", 16), ("EA", 64), ("EC", 64), ("HL", 32),
                 ("mask2", 64), ("abQ", 256), ("abC", 160)],
}
PLACE = {}
for (_b, _d), _l in PACK.items():
    _o = 0
    for _n, _w in _l:
        PLACE[_n] = (_b, _o, _w)
        _o += _w
    SCRATCH[_b] = _sb(_o, _d)
for _k in (0, 1, 2, 3, 4, 5, 7):
    SCRATCH["b%d" % _k] = ("psum", [128, 512], F32)
SCRATCH["b6"] = ("psum", [128, 1024], BF)
SEMAPHORES = ["mArr", "aArr", "bArr0", "bArr1", "tArr", "cArr0", "cArr1", "dArr"] + ["e%d" % i for i in range(NEV)]

OP = AluOpType
SR, AND = OP.logical_shift_right, OP.bitwise_and
FN = ActivationFunctionType
RND = 1.5 * 2.0 ** 23


def rank_program(g, core, T, topo):
    rank = T.rank_of(core)
    if rank is None:
        return
    cores = T.cores
    v, pe, sc, sy = g.vector, g.tensor, g.scalar, g.sync
    Q = {"v": v, "p": pe, "a": sc, "y": sy, "g": g}
    chips = []
    for c in cores:
        if topo.chip(c) not in chips:
            chips.append(topo.chip(c))
    partner = [c for c in cores if c != core and topo.chip(c) == topo.chip(core)][0]
    part = rank % 2
    lane = [[c for c in cores if topo.chip(c) == ch and topo.die(c) == topo.die(core)][0] for ch in chips]
    nl, me = len(lane), lane.index(core)
    order = [(me + d) % nl for d in range(1, nl)]
    early = [(me - d) % nl for d in (1, 2)]

    def A(name, a=0, b=None, step=1):
        buf, o, w = PLACE[name]
        b = w if b is None else b
        return T[buf][:, o + a:o + b:step] if step > 1 else T[buf][:, o + a:o + b]

    groups, waited, own = [], {}, []

    def ev(sem=None, n=0):
        if sem is None:
            sem = T.sem["e%d" % len(own)]
            own.append(sem)
        e = {"s": sem, "n": n, "k": len(groups)}
        groups.append(e)
        return e

    def inc(ins, e, n=1):
        ins.then_inc(e["s"], n)
        e["n"] += n

    def need(q, *es):
        for e in es:
            if waited.get((q, e["k"]), 0) < e["n"]:
                Q[q].wait_ge(e["s"], e["n"])
                waited[(q, e["k"])] = e["n"]

    def ts(e, out, in0, s1, s2, op0, op1=None):
        if op1 is None:
            inc(v.tensor_scalar(out, in0, s1, None, op0), e)
        else:
            inc(v.tensor_scalar(out, in0, s1, s2, op0, op1), e)

    def tt(e, out, in0, in1, op):
        inc(v.tensor_tensor(out, in0, in1, op), e)

    def cp(e, out, in_):
        inc(v.tensor_copy(out, in_), e)

    def fill(e, out, x):
        inc(v.memset(out, x), e)

    def act(e, out, in_, fn=FN.Copy, bias=0.0, scale=1.0):
        inc(sc.activation(out, in_, fn, bias=bias, scale=scale), e)

    def rnd(e, out, in0, unit, more=0.0):
        inc(v.tensor_scalar(out, in0, RND * unit, more - RND * unit, OP.add, OP.add), e)

    def scan(e, out, resets, in_, op):
        inc(v.tensor_tensor_scan(out, resets, in_, 0.0, OP.mult, op), e)

    def bits(m):
        return [b for b in range(16) if (m >> b) & 1]

    def send(members, src, at, dst, w, rsem):
        e = ev()
        ob = bits(topo.mask(core, lane[members[0]]))
        per = len(ob) // len(members)
        tr = []
        for n, (i, s) in enumerate(zip(members, at)):
            rid, pid, _ = topo.addr(lane[i])
            tr.append(RemoteDMATransfer(dst_ids=[DstId(rid=rid, pnc=pid)], dma_engine_mask=sum(1 << b for b in ob[n * per:(n + 1) * per]),
                                        remote_sem=rsem, src=src[:, s * w:(s + 1) * w], dst=dst[:, me * w:(me + 1) * w]))
            e["n"] += per
        g.remote_dma_fused(tr, local_sem=e["s"])
        return e

    leave = topo.mask(core, lane[order[0]])
    noff = len(bits(leave))
    aArr = ev(T.sem.aArr, noff)
    bArr = [ev(T.sem.bArr0, noff), ev(T.sem.bArr1, 2 * noff)]
    cArr = [ev(T.sem.cArr0, noff), ev(T.sem.cArr1, noff)]
    dArr = ev(T.sem.dArr, 3 * noff)
    full = topo.mask(core, partner)
    stay = full & ~leave
    prid, ppid, _ = topo.addr(partner)

    def exchange(buf, a, b, rsem, e, mask):
        g.remote_dma(buf[:, a:b], buf[:, a:b], rsem, e["s"], ppid, prid, mask)
        e["n"] += len(bits(mask))

    eIx = ev()
    inc(sy.dma_start(T.ix[:], T.idx[:]), eIx, 16)
    m0 = 2049 * part
    eM = []
    for h in range(MC):
        eM.append(ev())
        inc(sy.dma_start(T.winM[:, m0 + h * MW:m0 + (h + 1) * MW], T.mp[:, h * 8 * MW:(h + 1) * 8 * MW]), eM[h], 16)
    t0 = 8192 * part
    eT = [ev(), ev(), ev(), ev()]

    def load_table(q):
        inc(sy.dma_start(T.winT[:, t0 + 2048 * q:t0 + 2048 * q + 2048], T.tab[:, 2048 * q:2048 * q + 2048]), eT[q], 16)

    def iota(out, pattern, base, cm):
        e = ev()
        inc(g.iota(out, pattern, base, cm, allow_small_or_imprecise_dtypes=True), e)
        return e
    iI16 = iota(A("I16"), [[0, 4], [1, 16]], 0, 0)
    iJK = iota(A("JK"), [[1, 128]], 0, -1)
    iN2 = iota(A("N2f"), [[2, 80]], int(BIG), 0)
    iI128 = iota(A("I128"), [[1, 128]], 0, 0)
    iPI = iota(A("PI"), [[0, 2]], 0, 1)

    o1, o16 = PLACE["ones"][1], PLACE["I16"][1]
    eOne, eRep, eR0, eRow, eZ, eZd, eL, eLp, eN2 = [ev() for _ in range(9)]
    eRst, eI128m, eI128q, eU16 = [ev() for _ in range(4)]
    fill(eR0, T.row[0:2, 0:64], -7.5)
    fill(eOne, A("ones"), 0.125)
    for k in range(4):
        fill(eRep, T.rep[:, k:k + 1], k)
    need("v", iI16, eR0)
    ts(eRow, T.row[0:1, 0:64], T.pb[0:1, o16:o16 + 64], float(SZ), None, OP.mult)
    fill(eZ, T.zero[:], 0)
    need("v", iJK)
    ts(eL, A("Lt"), A("JK"), 0.0, BIG, OP.is_equal, OP.mult)
    ts(eL, A("Lu"), A("JK"), 0.0, 0.125, OP.is_gt, OP.mult)
    need("v", eL)
    tt(eLp, A("Lp"), A("Lt"), A("Lu"), OP.add)
    need("a", iI16)
    act(eRst, A("rst64"), A("I16"), FN.Sign)
    act(eU16, A("U16"), A("I16", 0, 16), scale=16.0)
    need("a", iI128)
    act(eI128m, A("I128m"), A("I128"), scale=0.125, bias=-0.9375)
    act(eI128q, A("I128q"), A("I128"), scale=0.125, bias=-7.9375)
    need("a", eZ)
    inc(sc.dma_start(T.winM[:, 2048:2049], T.zero[:, 0:1]), eZd, 16)

    def rank_bias():
        e = ev()
        inc(pe.matmul(T.b0[:, 0:64], T.pb[0:2, o1:o1 + 128], T.row[0:2, 0:64], True, False), e)
        return e

    def rank_mm(E, e):
        inc(pe.matmul(T.b0[:, 0:64], A("Lp"), A(E), False, False), e)
        for d in (1, 2, 3):
            inc(pe.matmul(T.b0[:, 16 * d:64], A("ones"), A(E, 0, 64 - 16 * d), False, d == 3), e)

    need("p", eOne, eRow)
    eRA = rank_bias()

    need("v", eIx, eRep)
    e1, eEA, e2, e3, e4, s2, s3, s4 = [ev() for _ in range(8)]
    ts(e1, A("bI"), T.ix[:], 19, None, SR)
    need("v", e1)
    tt(eEA, A("EA"), A("bI").indirect(T.rep[:, 0:4]), A("I16"), OP.is_equal)
    need("p", eLp, eEA)
    rank_mm("EA", eRA)
    ts(e2, A("iG"), T.ix[:], 14, None, AND)
    ts(e2, A("iPart"), T.ix[:], 18, 1, SR, AND)
    ts(e2, A("iCl"), T.ix[:], 4, MW - 1, SR, AND)
    ts(e2, A("iCh"), T.ix[:], 7, 2048 - MW, SR, AND)
    need("v", iN2)
    cp(eN2, T.N2h[:], A("N2f"))
    need("v", eRst, eRA)
    scan(s2, A("SA"), A("rst64"), T.b0[:, 0:64], OP.max)
    need("v", e2)
    ts(e3, A("dP"), A("iPart"), 2049.0, -2048.0, OP.mult, OP.add)
    tt(e3, A("dC"), A("iCl"), A("iCh"), OP.add)
    need("v", s2)
    rnd(s3, A("c16A"), A("SA", 15, 64, 16), 2)
    tt(s4, A("mA"), A("SA", 15, 64, 16), A("iG"), OP.add)
    need("v", e3)
    tt(e4, A("delta"), A("dC"), A("dP"), OP.add)
    need("v", eN2, s3, e4, s4, eI128m)
    eSA = ev()
    for k in range(4):
        b = ev()
        l, r = T.lA[:, 128 * k:128 * k + 128], T.rA[:, 80 * k:80 * k + 80]
        ts(b, r, T.N2h[:], A("c16A", k, k + 1), A("delta", k, k + 1), OP.is_equal, OP.mult)
        ts(b, l, A("I128m"), A("c16A", k, k + 1), A("mA", k, k + 1), OP.add, OP.is_equal)
        need("p", b)
        inc(pe.matmul(T.b1[:, 0:80], l, r, k == 0, k == 3), eSA)
    need("v", eSA)
    eA1, eA2 = ev(), ev()
    ts(eA1, T.sendA[:], T.b1[:, 0:80], 2048.0, None, OP.add)
    ts(eA2, T.offA[:, W * me:W * me + W], T.b1[:, W * me:W * me + W], 2048.0, None, OP.add)

    eMx = ev()
    for h, mask in ((0, full), (1, full), (2, stay)):
        need("g", eM[h])
        exchange(T.winM, m0 + h * MW, m0 + (h + 1) * MW, T.sem.mArr, eMx, mask)
    need("g", eA1)
    locA = send(order, T.sendA, order, T.offA, W, T.sem.aArr)
    need("g", *eM)
    exchange(T.winM, m0 + 3 * MW, m0 + 2048, T.sem.mArr, eMx, full)
    mapsent = ev(T.sem.mArr, eMx["n"])

    need("y", locA)
    load_table(0)
    load_table(1)
    need("y", eT[0], eT[1])
    load_table(2)

    iI160 = iota(A("I160"), [[1, 160]], 0, 0)
    iI16b = iota(A("I16b"), [[0, 10], [1, 16]], 0, 0)
    iTC = iota(A("TC"), [[0, 4], [NT, 16]], int(BIG2), 0)
    iZ4 = iota(A("Z4"), [[1, 8], [0, 4]], 0, 0)

    f1, f2, f3, f4, f5, f6, f7 = [ev() for _ in range(7)]
    k1, k2, kS, kT, kI = ev(), ev(), ev(), ev(), ev()
    ts(f1, A("a0"), A("SA", 15, 64, 16), -7.0 - BIG, None, OP.add)
    ts(f1, A("iNl"), T.ix[:], 1, None, AND)
    ts(f1, A("iNh"), T.ix[:], 13, 7, SR, AND)
    need("v", iPI, iI128)
    ts(k1, A("P15"), A("PI", 0, 1), 15, None, AND)
    need("v", f1)
    rnd(f2, A("u16"), A("a0"), 16)
    ts(f2, A("n1"), A("iNl"), 8.0, None, OP.mult)
    need("v", k1)
    cp(k2, A("PF", 0, 1), A("P15"))
    need("v", f2)
    tt(f3, A("pl"), A("a0"), A("u16"), OP.subtract)
    tt(f4, A("n2"), A("n1"), A("iNh"), OP.add)
    need("v", k2)
    ts(kT, A("S16a"), A("I16", 0, 16), A("PF", 0, 1), None, OP.is_equal)
    ts(kT, A("S16b"), A("I128", 1, 17), A("PF", 0, 1), None, OP.is_equal)
    need("v", f4)
    tt(f5, A("qc"), A("n2"), A("u16"), OP.add)
    need("v", kT)
    tt(kS, A("S16"), A("S16a"), A("S16b"), OP.subtract)
    need("v", f3, eI128q)
    for k in (0, 1):
        ts(f6, T.lQ[:, 128 * k:128 * k + 128], A("I128q"), A("pl", k, k + 1), None, OP.is_equal)
    ts(kI, A("ident"), A("JK"), 0.0, None, OP.is_equal)
    need("v", f5, iI160)
    for k in range(4):
        ts(f6, T.rQ[:, 160 * k:160 * k + 160], A("I160"), A("qc", k, k + 1), None, OP.is_equal)
    need("a", f3, eI128q)
    fa = ev()
    for k in (2, 3):
        act(fa, A("abQ", 128 * (k - 2), 128 * (k - 1)), A("I128q"), FN.Abs, bias=A("pl", k, k + 1), scale=-1.0)
    need("a", fa)
    for k in (2, 3):
        act(f7, T.lQ[:, 128 * k:128 * k + 128], A("abQ", 128 * (k - 2), 128 * (k - 1)), FN.Relu, bias=1.0, scale=-8.0)
    need("p", f6, f7, kI)
    eQ, eTr, eTk, eKeep = ev(), ev(), ev(), ev()
    for k in range(4):
        inc(pe.matmul(T.b2[:, 0:160], T.lQ[:, 128 * k:128 * k + 128], T.rQ[:, 160 * k:160 * k + 160], k == 0, k == 3), eQ)
    for k in range(4):
        inc(pe.transpose(T.b6[:, 128 * k:128 * k + 128], T.lQ[:, 128 * k:128 * k + 128], A("ident")), eTr)

    for q in ("v", "a"):
        need(q, mapsent, aArr, eA1, eA2, eZd, *eM)
    need("p", kS)
    locB, eB2 = [], ev()

    def fetch(members, bank, before=()):
        e = ev()
        for n, i in enumerate(members):
            for u in (0, 1):
                b = ev()
                a, o = SZ * i + 128 * u, W * i + 8 * u
                (cp, act)[u](b, T.G[:, a:a + 128], T.winM[:, 0:NM].indirect(T.offA[:, o:o + 8]))
                need("p", b, *before)
                inc(pe.matmul(bank[:, 32 * n + 16 * u:32 * n + 16 * u + 16], T.G[:, a:a + 128], A("S16"), True, True), e)
        return e

    def answer(q, e, members, bank, o, rsem):
        c, n = ev(), len(members)
        need(q, e)
        (cp if q == "v" else act)(c, T.sendB[:, 32 * o:32 * (o + n)], bank[:, 0:32 * n])
        need("g", c)
        locB.append(send(members, T.sendB, [o + k for k in range(n)], T.landB, 32, rsem))
        return c

    m = [order[0:2], order[2:3], order[3:4]]
    b0 = fetch(m[0], T.b3)
    b1 = fetch(m[1], T.b4)
    c0 = answer("v", b0, m[0], T.b3, 0, T.sem.bArr0)
    b2 = fetch(m[2], T.b7)
    answer("a", b1, m[1], T.b4, 2, T.sem.bArr1)
    answer("a", b2, m[2], T.b7, 3, T.sem.bArr1)
    b3 = fetch([me], T.b3, [c0])
    need("v", b3)
    cp(eB2, T.landB[:, 32 * me:32 * me + 32], T.b3[:, 0:32])
    need("a", eQ)
    act(eKeep, A("keep"), T.b2[:, 0:160], scale=-1.0, bias=1.0)
    need("a", eTr)
    act(eTk, T.Tk[:], T.b6[:, 0:512])

    need("y", *locB)
    load_table(3)
    eTx = ev()
    for q in range(4):
        need("g", eT[q])
        exchange(T.winT, t0 + 2048 * q, t0 + 2048 * q + 2048, T.sem.tArr, eTx, full)

    k3, k3r, k4, kA, kR = ev(), ev(), ev(), ev(), ev()
    need("a", iI16b)
    act(kR, A("HL"), A("I16b", 0, 32), scale=0.0)
    act(kA, A("I16m"), A("I16b", 0, 128), scale=0.125, bias=-0.9375)
    fill(k3r, T.row[0:2, 128:192], 4.0)
    ts(k4, A("P7"), A("PI", 0, 1), 7, None, AND)
    ts(k4, A("PS3"), A("PI", 0, 1), 3, None, SR)
    ts(k4, A("P3"), A("PI"), 3, None, AND)
    need("v", eU16)
    for k in range(4):
        ts(k3, A("mask2", 16 * k, 16 * k + 16), A("U16"), A("u16", k, k + 1), BIG2, OP.is_equal, OP.mult)
    need("v", k3r)
    fill(k3, T.row[0:1, 128:192], -NT * 4.0)
    need("v", k4, k3, iTC, iI16b, iZ4)
    need("p", k3)
    eDm = ev()
    inc(pe.matmul(T.b5[:, 0:64], T.pb[0:2, o1:o1 + 128], T.row[0:2, 128:192], True, False), eDm)
    inc(pe.matmul(T.b5[:, 0:64], A("ident"), A("mask2"), False, False), eDm)
    eRC = rank_bias()
    k5, k6 = ev(), ev()
    cp(k5, A("PF", 1, 2), A("P7"))
    cp(k5, A("PF", 2, 3), A("PS3"))
    cp(k6, T.repF[:], A("P3"))
    need("v", k5)
    ts(k6, T.lF[:], A("I16b", 0, 128), A("PF", 2, 3), None, OP.is_equal)
    ts(k6, A("Z0"), A("Z4"), A("PF", 1, 2), None, OP.is_equal)

    x2, x3, x4, x6, x7, x8, x9, x10, x12, y5, y7 = [ev() for _ in range(11)]
    need("v", eB2, eKeep, kR)
    for p in (0, 1):
        blocks = [i for i in range(nl) if (i in early) == (p == 0)]
        runs = []
        for i in blocks:
            if runs and runs[-1][1] == i:
                runs[-1][1] = i + 1
            else:
                runs.append([i, i + 1])
        need("v", bArr[p])
        for a, b in runs:
            scan(x2, A("SX", 32 * a, 32 * b), A("keep", 32 * a, 32 * b), T.landB[:, 32 * a:32 * b], OP.add)
    need("v", x2)
    rnd(x3, A("HL", 0, 10), A("SX", 15, 160, 16), 512)
    need("v", x3)
    tt(x4, A("HL", 16, 26), A("SX", 15, 160, 16), A("HL", 0, 10), OP.subtract)
    for w, e in ((0, x3), (1, x4)):
        need("p", e, eTk)
        for k in range(4):
            inc(pe.matmul(T.b5[:, 16 * k:16 * k + 16], T.Tk[:, 128 * k:128 * k + 128], A("HL", 16 * w, 16 * w + 16), False, w == 1 and k == 3), eDm)
    need("v", eDm)
    scan(x6, A("SD"), A("rst64"), T.b5[:, 0:64], OP.max)
    need("v", x6)
    rnd(x7, A("tU"), A("SD", 15, 64, 16), NT)
    need("v", x7)
    eEC = ev()
    tt(eEC, A("EC"), A("tU").indirect(T.rep[:, 0:4]), A("TC"), OP.is_equal)
    need("p", eEC)
    rank_mm("EC", eRC)
    tt(x8, A("lc"), A("SD", 15, 64, 16), A("tU"), OP.subtract)
    need("v", x8)
    rnd(x9, A("hi2"), A("lc"), 64, -64.0)
    need("v", eRC)
    scan(x12, A("SC"), A("rst64"), T.b0[:, 0:64], OP.max)
    need("v", x9)
    tt(x10, A("lo2"), A("lc"), A("hi2"), OP.subtract)
    need("v", x12)
    rnd(y5, A("c16C"), A("SC", 15, 64, 16), 2)
    need("v", x10)
    ts(y7, A("lon"), A("lo2"), -1.0, None, OP.mult)
    need("v", y5, kA)
    sa, sb = ev(), [ev(), ev()]
    need("a", y5)
    for k in (2, 3):
        act(sa, A("abC", 80 * (k - 2), 80 * (k - 1)), A("N2f"), FN.Abs, bias=A("c16C", k, k + 1), scale=-1.0)
    need("a", sa, x10, y7)
    for k in (2, 3):
        act(sb[k - 2], T.rC[:, 160 * k + 80:160 * k + 160], A("abC", 80 * (k - 2), 80 * (k - 1)), FN.Relu,
            bias=A("lo2", k, k + 1), scale=A("lon", k, k + 1))
    eSC = ev()
    for k in range(4):
        b = ev()
        l, r = T.lC[:, 128 * k:128 * k + 128], [T.rC[:, 160 * k + 80 * q:160 * k + 80 * q + 80] for q in (0, 1)]
        ts(b, r[0], T.N2h[:], A("c16C", k, k + 1), A("hi2", k, k + 1), OP.is_equal, OP.mult)
        if k < 2:
            ts(b, r[1], T.N2h[:], A("c16C", k, k + 1), A("lo2", k, k + 1), OP.is_equal, OP.mult)
        ts(b, l, A("I16m"), A("c16C", k, k + 1), A("SC", 16 * k + 15, 16 * k + 16), OP.add, OP.is_equal)
        need("p", b)
        for q in (0, 1):
            if k > 1 and q == 1:
                need("p", sb[k - 2])
            inc(pe.matmul(T.b1[:, 0:80], l, r[q], k == 0 and q == 0, k == 3 and q == 1), eSC)
    need("v", eSC)
    eCs1, eCs2 = ev(), ev()
    ts(eCs1, T.sendC[:], T.b1[:, 0:80], NT / 2 - 0.5, None, OP.add)
    ts(eCs2, T.offC[:, W * me:W * me + W], T.b1[:, W * me:W * me + W], NT / 2 - 0.5, None, OP.add)
    need("g", eCs1)
    send(order[2:4], T.sendC, order[2:4], T.offC, W, T.sem.cArr0)
    send(order[0:2], T.sendC, order[0:2], T.offC, W, T.sem.cArr1)

    y1, y2, y3, y4 = ev(), ev(), ev(), ev()
    ts(y1, A("slotC"), A("SC", 15, 64, 16), 8.0, 7.5 - 8.0 * BIG, OP.mult, OP.add)
    need("v", y1, k6)
    tt(y2, T.rF[:], A("slotC").indirect(T.repF[:, 0:2]), A("Z0"), OP.mult)
    need("p", y2)
    inc(pe.matmul(T.b3[:, 0:32], T.lF[:], T.rF[:], True, True), y3)
    need("v", y3)
    cp(y4, T.offF[:], T.b3[:, 0:32])

    eTa = ev(T.sem.tArr, eTx["n"])
    for q in ("v", "a"):
        need(q, eTa, eCs2, *eT)

    def serve(i, dst, e):
        for n in (0, 1):
            a = SZ * i + 128 * n
            src = T.winT[:, 0:NT].indirect(T.offC[:, W * i + 8 * n:W * i + 8 * n + 8])
            (cp, act)[n](e[n], dst[:, a:a + 128], src)

    for p, members in enumerate((order[0:1], order[1:2], order[2:4])):
        for q in ("v", "a"):
            need(q, cArr[p // 2])
        e = [ev(), ev()]
        if len(members) == 1:
            serve(members[0], T.sendD, e)
        else:
            for n, i in enumerate(members):
                src = T.winT[:, 0:NT].indirect(T.offC[:, W * i:W * i + W])
                (cp, act)[n](e[n], T.sendD[:, SZ * i:SZ * i + SZ], src)
        need("g", *e)
        send(members, T.sendD, members, T.landD, SZ, T.sem.dArr)
    eD = [ev(), ev()]
    serve(me, T.landD, eD)

    for q in ("v", "a"):
        need(q, dArr, y4, *eD)
    eY1, eY2, eS1, eS2 = ev(), ev(), ev(), ev()
    cp(eY1, T.yo[:, 0:256], T.landD[:, 0:1280].indirect(T.offF[:, 0:16]))
    act(eY2, T.yo[:, 256:512], T.landD[:, 0:1280].indirect(T.offF[:, 16:32]))
    need("y", eY1)
    inc(sy.dma_start(T.y[:, 0:256], T.yo[:, 0:256]), eS1, 16)
    need("a", eY2)
    inc(sc.dma_start(T.y[:, 256:512], T.yo[:, 256:512]), eS2, 16)
    need("y", eS1)
    need("a", eS2)
    done = set(k for (_, k), n in waited.items() if n == groups[k]["n"])
    for e in groups:
        if e["n"] > 0 and e["k"] not in done:
            need("g", e)
